import numpy as np
import ml_dtypes


def mxq(x, axis, fmt="e4m3"):
    dtype, down = {"e4m3": (ml_dtypes.float8_e4m3fn, 7), "e5m2": (ml_dtypes.float8_e5m2, 14)}[fmt]
    v = np.moveaxis(np.asarray(x, np.float32).astype(ml_dtypes.bfloat16).astype(np.float64), axis, -1)
    blocks = v.reshape(v.shape[:-1] + (-1, 32))
    amax = np.abs(blocks).max(-1, keepdims=True)
    byte = np.maximum(np.where(amax > 0, np.frexp(amax)[1] - 1 + 127, 0) - down, 1)
    scale = np.exp2(byte - 127.0)
    codes = (blocks / scale).astype(np.float32).astype(dtype).astype(np.float64)
    return np.moveaxis((codes * scale).reshape(v.shape), -1, axis)


WIDE = False


def mx_kscale(k):
    if not WIDE:
        return np.ones(k)
    levels = np.array([10, -10, 5, -5, 0])
    if k % 512:
        return np.exp2(np.random.permutation(np.resize(levels, k // 32))).repeat(32)
    a = np.empty((k // 512, 16))
    for p in range(k // 512):
        a[p, :8] = np.random.permutation(np.resize(levels, 8))
        for g in range(8):
            far = levels[np.abs(levels - a[p, g]) >= 10]
            a[p, g + 8] = far[np.random.randint(len(far))]
    return np.exp2(a.ravel()).repeat(32)


def f64(x):
    return np.asarray(x).astype(np.float64)


def striped(idx):
    return np.tile(idx.reshape(-1, 16).T, (8, 1)).astype(np.uint16)


def unstriped(offs):
    return offs[:16].T.reshape(-1).astype(np.int64)


def striped8(idx):
    return np.concatenate([v.reshape(-1, 16).T for v in idx]).astype(np.uint16)


def unstriped8(offs):
    return np.stack([offs[16 * g:16 * g + 16].T.reshape(-1) for g in range(8)]).astype(np.int64)


E2M1 = np.array([0.0, 0.5, 1.0, 1.5, 2.0, 3.0, 4.0, 6.0, -0.0, -0.5, -1.0, -1.5, -2.0, -3.0, -4.0, -6.0])


def pack_weight(w, fmt):
    k, n = w.shape
    w = f64(np.asarray(w, np.float32).astype(ml_dtypes.bfloat16)).reshape(k // 32, 32, n)
    amax = np.abs(w).max(1)
    if fmt == "e4m3":
        byte = np.frexp(amax)[1] - 1 + 127 - 7
    else:
        mant, ex = np.frexp(amax / 6.0)
        byte = np.where(mant > 0.5, ex, ex - 1) + 127
    byte = np.clip(np.where(amax > 0, byte, 1), 1, 254)
    scaled = (w * np.exp2(127.0 - byte)[:, None, :]).reshape(k, n).astype(np.float32)
    by_word = np.ascontiguousarray(scaled.reshape(k // 512, 128, 4, n).transpose(0, 1, 3, 2))
    if fmt == "e4m3":
        words = by_word.astype(ml_dtypes.float8_e4m3fn).view(np.uint8)
    else:
        c = by_word.astype(ml_dtypes.float4_e2m1fn).view(np.uint8) & 0xF
        words = (c[..., 0::2] | (c[..., 1::2] << 4)).reshape(k // 512, 128, 2 * n)
    return np.ascontiguousarray(words), np.ascontiguousarray(byte.astype(np.uint8).reshape(k // 512, 16, n))


def unpack_weight(words, scales, fmt):
    g, _, n = scales.shape
    words = np.ascontiguousarray(words).reshape(g, 128, n, -1)
    if fmt == "e4m3":
        vals = words.view(ml_dtypes.float8_e4m3fn).astype(np.float64)
    else:
        nib = np.empty((g, 128, n, 4), np.uint8)
        nib[..., 0::2] = words & 0xF
        nib[..., 1::2] = words >> 4
        vals = E2M1[nib]
    vals = vals * np.repeat(np.exp2(scales.astype(np.float64) - 127.0), 8, axis=1)[..., None]
    return vals.transpose(0, 1, 3, 2).reshape(g * 512, n)


def pack_table(v):
    words, scales = pack_weight(v, "e4m3")
    return np.concatenate([words.reshape(words.shape[0], -1), scales.reshape(scales.shape[0], -1)], axis=1)


def unpack_table(tab):
    g, t = tab.shape[0], tab.shape[1] // 528
    return unpack_weight(tab[:, :512 * t].reshape(g, 128, t, 4), tab[:, 512 * t:].reshape(g, 16, t), "e4m3")


K, M, T, S = 512, 512, 1024, 512


def setup_inputs():
    n = np.random.standard_normal
    s = mx_kscale(K)[:, None]
    return {
        "tab": pack_table(n((K, T)) * s),
        "w": (n((K, M)) / np.sqrt(K) / s).astype(np.float32),
        "wgo": np.repeat(np.random.uniform(0.5, 2.0, (8, S)), 16, axis=0).astype(np.float32),
        "offs": striped(np.random.permutation(T)[:S]),
        "offs2": striped8(np.stack([np.random.permutation(T)[:S] for _ in range(8)])),
    }


def reference(tab, w, wgo, offs, offs2):
    tab_ = unpack_table(tab)[:, unstriped(offs)]
    w_ = mxq(f64(w), 0, "e4m3")
    y = w_.T @ tab_
    place = unstriped8(offs2)[np.arange(M) % 128 // 16]
    out = np.zeros((M, T))
    out[np.arange(M)[:, None], place] = f64(wgo)[np.arange(M) % 128] * (y)
    return out

@@ -1,0 +1,110 @@
+from contextlib import ExitStack
+
+import concourse.mybir as mybir
+
+K, M, T, S = 512, 512, 1024, 512
+FLOPS = 2 * K * M * S
+
+F32 = mybir.dt.float32
+BF16 = mybir.dt.bfloat16
+I32 = mybir.dt.int32
+U32 = mybir.dt.uint32
+U16 = mybir.dt.uint16
+U8 = mybir.dt.uint8
+FP8X4 = mybir.dt.float8_e4m3fn_x4
+
+P = 128
+PACK = 4
+M_TILES = M // P
+HALF = S // 2
+LIST_COLS = S // 16
+HALF_COLS = LIST_COLS // 2
+
+
+def tile_list_tabhs_none_kernel(tc, tab, w, wgo, offs, offs2, out):
+    nc = tc.nc
+    mult = mybir.AluOpType.mult
+
+    tab_words = tab[0, 0 : 4 * P * T].rearrange("(p n) -> p n", p=P)
+    tab_scales = tab[0, 4 * P * T :].rearrange("(q n) -> q n", q=16)
+    w_rows = w.rearrange("(p j) c -> p j c", j=PACK)
+
+    with ExitStack() as ctx:
+        lists = ctx.enter_context(tc.tile_pool(name="lists", bufs=1))
+        keep = ctx.enter_context(tc.tile_pool(name="keep", bufs=1))
+        psum = ctx.enter_context(tc.psum_pool(name="psum", bufs=1))
+
+        pick = lists.tile([P, LIST_COLS], U16, name="pick")
+        place = lists.tile([P, LIST_COLS], U16, name="place")
+
+        words = keep.tile([P, T], U32, name="words", align_bytes=64)
+        scales = keep.tile([P, T], U8, name="scales", align_bytes=64)
+        weights_of_place = keep.tile([P, S], F32, name="weights_of_place", align_bytes=64)
+
+        nc.gpsimd.memset(scales[:].bitcast(I32), 0)
+        nc.gpsimd.dma_start(out=weights_of_place[:], in_=wgo)
+        nc.sync.dma_start(pick[:], offs)
+        for quad in range(4):
+            nc.sync.dma_start(
+                out=scales[32 * quad : 32 * quad + 4, :].bitcast(I32),
+                in_=tab_scales[4 * quad : 4 * quad + 4, :].bitcast(I32),
+            )
+        w_raw_0 = keep.tile([P, PACK, 1 * P], F32, name="w_raw_0", align_bytes=64)
+        nc.scalar.dma_start(out=w_raw_0[:], in_=w_rows[:, :, 0 * P : 1 * P])
+        nc.sync.dma_start(out=words[:].bitcast(I32), in_=tab_words.bitcast(I32))
+        w_raw_1 = keep.tile([P, PACK, 3 * P], F32, name="w_raw_1", align_bytes=64)
+        nc.sync.dma_start(out=w_raw_1[:], in_=w_rows[:, :, 1 * P : 4 * P])
+        nc.sync.dma_start(place[:], offs2)
+        windows = []
+        for m in range(M_TILES):
+            window = keep.tile([P, T], F32, name=f"window{m}", align_bytes=64)
+            zero_engine = nc.vector if m < 2 else nc.gpsimd
+            zero_engine.memset(window[:], 0.0)
+            windows.append(window)
+
+        def quantize_w(m, raw):
+            grouped = keep.tile([P, P, PACK], BF16, name=f"w_grouped{m}", align_bytes=64)
+            nc.scalar.copy(grouped[:], raw.rearrange("p j c -> p c j"))
+            codes = keep.tile([P, P], U32, name=f"w_codes{m}", align_bytes=64)
+            code_scales = keep.tile([P, P], U8, name=f"w_scales{m}", align_bytes=64)
+            nc.vector.quantize_mx(
+                out=codes[:].bitcast(FP8X4),
+                scales=code_scales[:],
+                in_=grouped[:].rearrange("p c j -> p (c j)"),
+            )
+            return codes, code_scales
+
+        halves = [pick[:, h * HALF_COLS : (h + 1) * HALF_COLS] for h in range(2)]
+        picked_scales = [keep.tile([P, HALF], U8, name=f"picked_scales{h}", align_bytes=64) for h in range(2)]
+        picked_words = [keep.tile([P, HALF], U32, name=f"picked_words{h}", align_bytes=64) for h in range(2)]
+        w_tiles = []
+        w_tiles.append(quantize_w(0, w_raw_0[:]))
+        nc.vector.tensor_copy(picked_scales[0][:], scales[:].indirect(halves[0]))
+        nc.vector.tensor_copy(picked_words[0][:], words[:].indirect(halves[0]))
+        nc.vector.tensor_copy(picked_scales[1][:], scales[:].indirect(halves[1]))
+        nc.vector.tensor_copy(picked_words[1][:], words[:].indirect(halves[1]))
+        w_tiles.append(quantize_w(1, w_raw_1[:, :, 0:P]))
+        w_tiles.append(quantize_w(2, w_raw_1[:, :, P : 2 * P]))
+        w_tiles.append(quantize_w(3, w_raw_1[:, :, 2 * P : 3 * P]))
+        for m in range(M_TILES):
+            codes, code_scales = w_tiles[m]
+            for h in range(2):
+                bank = psum.tile([P, HALF], F32, name=f"bank{m}_{h}")
+                nc.tensor.matmul_mx(
+                    out=bank[:],
+                    lhsT=codes[:].bitcast(FP8X4),
+                    lhsT_scale=code_scales[:],
+                    rhs=picked_words[h][:].bitcast(FP8X4),
+                    rhs_scale=picked_scales[h][:],
+                    start=True,
+                    stop=True,
+                )
+                y = keep.tile([P, HALF], F32, name=f"y{m}_{h}", align_bytes=64)
+                nc.scalar.copy(y[:], bank[:])
+                nc.vector.tensor_tensor(
+                    windows[m][:].indirect(place[:, h * HALF_COLS : (h + 1) * HALF_COLS]),
+                    y[:],
+                    weights_of_place[:, h * HALF : (h + 1) * HALF],
+                    mult,
+                )
+            nc.sync.dma_start(out=out[m * P : (m + 1) * P, :], in_=windows[m][:])

@@ -40,33 +40,37 @@ def tile_list_tabhs_none_kernel(tc, tab, w, wgo, offs, offs2, out):
         words = keep.tile([P, T], U32, name="words", align_bytes=64)
         scales = keep.tile([P, T], U8, name="scales", align_bytes=64)
         weights_of_place = keep.tile([P, S], F32, name="weights_of_place", align_bytes=64)
+        w_raw_0 = keep.tile([P, PACK, P], F32, name="w_raw_0", align_bytes=64)
+        w_raw_1 = keep.tile([P, PACK, P], F32, name="w_raw_1", tag="raw_1", align_bytes=64)
+        w_raw_23 = keep.tile([P, PACK, 2 * P], F32, name="w_raw_23", tag="raw_23", align_bytes=64)
 
         nc.gpsimd.memset(scales[:].bitcast(I32), 0)
-        nc.gpsimd.dma_start(out=weights_of_place[:], in_=wgo)
         nc.sync.dma_start(pick[:], offs)
+        nc.scalar.dma_start(out=w_raw_0[:], in_=w_rows[:, :, 0:P])
+        nc.sync.dma_start(place[:], offs2)
+        nc.scalar.dma_start(out=words[:].bitcast(I32), in_=tab_words.bitcast(I32))
         for quad in range(4):
             nc.sync.dma_start(
                 out=scales[32 * quad : 32 * quad + 4, :].bitcast(I32),
                 in_=tab_scales[4 * quad : 4 * quad + 4, :].bitcast(I32),
             )
-        w_raw_0 = keep.tile([P, PACK, 1 * P], F32, name="w_raw_0", align_bytes=64)
-        nc.scalar.dma_start(out=w_raw_0[:], in_=w_rows[:, :, 0 * P : 1 * P])
-        nc.sync.dma_start(out=words[:].bitcast(I32), in_=tab_words.bitcast(I32))
-        w_raw_1 = keep.tile([P, PACK, 3 * P], F32, name="w_raw_1", align_bytes=64)
-        nc.sync.dma_start(out=w_raw_1[:], in_=w_rows[:, :, 1 * P : 4 * P])
-        nc.sync.dma_start(place[:], offs2)
+        nc.sync.dma_start(out=weights_of_place[:], in_=wgo)
+        nc.sync.dma_start(out=w_raw_1[:], in_=w_rows[:, :, P : 2 * P])
+        nc.sync.dma_start(out=w_raw_23[:], in_=w_rows[:, :, 2 * P : 4 * P])
         windows = []
-        for m in range(M_TILES):
-            window = keep.tile([P, T], F32, name=f"window{m}", align_bytes=64)
-            zero_engine = nc.vector if m < 2 else nc.gpsimd
-            zero_engine.memset(window[:], 0.0)
+        for i in range(3):
+            window = keep.tile([P, T], F32, name=f"window{i}", align_bytes=64)
+            nc.vector.memset(window[:], 0.0)
             windows.append(window)
 
-        def quantize_w(m, raw):
-            grouped = keep.tile([P, P, PACK], BF16, name=f"w_grouped{m}", align_bytes=64)
+        def interleave(name, raw, width):
+            grouped = keep.tile([P, width, PACK], BF16, name=f"w_grouped{name}", align_bytes=64)
             nc.scalar.copy(grouped[:], raw.rearrange("p j c -> p c j"))
-            codes = keep.tile([P, P], U32, name=f"w_codes{m}", align_bytes=64)
-            code_scales = keep.tile([P, P], U8, name=f"w_scales{m}", align_bytes=64)
+            return grouped
+
+        def quantize(name, grouped, width):
+            codes = keep.tile([P, width], U32, name=f"w_codes{name}", align_bytes=64)
+            code_scales = keep.tile([P, width], U8, name=f"w_scales{name}", align_bytes=64)
             nc.vector.quantize_mx(
                 out=codes[:].bitcast(FP8X4),
                 scales=code_scales[:],
@@ -74,37 +78,51 @@ def tile_list_tabhs_none_kernel(tc, tab, w, wgo, offs, offs2, out):
             )
             return codes, code_scales
 
-        halves = [pick[:, h * HALF_COLS : (h + 1) * HALF_COLS] for h in range(2)]
-        picked_scales = [keep.tile([P, HALF], U8, name=f"picked_scales{h}", align_bytes=64) for h in range(2)]
-        picked_words = [keep.tile([P, HALF], U32, name=f"picked_words{h}", align_bytes=64) for h in range(2)]
-        w_tiles = []
-        w_tiles.append(quantize_w(0, w_raw_0[:]))
-        nc.vector.tensor_copy(picked_scales[0][:], scales[:].indirect(halves[0]))
-        nc.vector.tensor_copy(picked_words[0][:], words[:].indirect(halves[0]))
-        nc.vector.tensor_copy(picked_scales[1][:], scales[:].indirect(halves[1]))
-        nc.vector.tensor_copy(picked_words[1][:], words[:].indirect(halves[1]))
-        w_tiles.append(quantize_w(1, w_raw_1[:, :, 0:P]))
-        w_tiles.append(quantize_w(2, w_raw_1[:, :, P : 2 * P]))
-        w_tiles.append(quantize_w(3, w_raw_1[:, :, 2 * P : 3 * P]))
-        for m in range(M_TILES):
-            codes, code_scales = w_tiles[m]
-            for h in range(2):
-                bank = psum.tile([P, HALF], F32, name=f"bank{m}_{h}")
-                nc.tensor.matmul_mx(
-                    out=bank[:],
-                    lhsT=codes[:].bitcast(FP8X4),
-                    lhsT_scale=code_scales[:],
-                    rhs=picked_words[h][:].bitcast(FP8X4),
-                    rhs_scale=picked_scales[h][:],
-                    start=True,
-                    stop=True,
-                )
-                y = keep.tile([P, HALF], F32, name=f"y{m}_{h}", align_bytes=64)
-                nc.scalar.copy(y[:], bank[:])
-                nc.vector.tensor_tensor(
-                    windows[m][:].indirect(place[:, h * HALF_COLS : (h + 1) * HALF_COLS]),
-                    y[:],
-                    weights_of_place[:, h * HALF : (h + 1) * HALF],
-                    mult,
-                )
-            nc.sync.dma_start(out=out[m * P : (m + 1) * P, :], in_=windows[m][:])
+        picked_scales = keep.tile([P, S], U8, name="picked_scales", align_bytes=64)
+        picked_words = keep.tile([P, S], U32, name="picked_words", align_bytes=64)
+
+        def product(name, codes, code_scales, lo, hi, tag):
+            bank = psum.tile([P, hi - lo], F32, name=f"bank{name}")
+            nc.tensor.matmul_mx(
+                out=bank[:],
+                lhsT=codes.bitcast(FP8X4),
+                lhsT_scale=code_scales,
+                rhs=picked_words[:, lo:hi].bitcast(FP8X4),
+                rhs_scale=picked_scales[:, lo:hi],
+                start=True,
+                stop=True,
+            )
+            y = keep.tile([P, hi - lo], F32, name=f"y{name}", tag=tag, align_bytes=64)
+            nc.scalar.copy(y[:], bank[:])
+            return y
+
+        def scatter(window, y, lo, hi):
+            nc.vector.tensor_tensor(
+                window[:].indirect(place[:, lo // 16 : hi // 16]),
+                y[:],
+                weights_of_place[:, lo:hi],
+                mult,
+            )
+
+        nc.vector.tensor_copy(picked_scales[:], scales[:].indirect(pick[:]))
+        c0, s0 = quantize("0", interleave("0", w_raw_0[:], P), P)
+        for h in range(2):
+            nc.vector.tensor_copy(
+                picked_words[:, h * HALF : (h + 1) * HALF],
+                words[:].indirect(pick[:, h * HALF_COLS : (h + 1) * HALF_COLS]),
+            )
+        y0a = product("0a", c0[:], s0[:], 0, HALF, "y0a")
+        scatter(windows[0], y0a, 0, HALF)
+        c1, s1 = quantize("1", interleave("1", w_raw_1[:], P), P)
+        y0b = product("0b", c0[:], s0[:], HALF, S, "raw_1")
+        scatter(windows[0], y0b, HALF, S)
+        nc.sync.dma_start(out=out[0:P, :], in_=windows[0][:])
+        c23, s23 = quantize("23", interleave("23", w_raw_23[:], 2 * P), 2 * P)
+        y1 = product("1", c1[:], s1[:], 0, S, "raw_23")
+        scatter(windows[1], y1, 0, S)
+        nc.sync.dma_start(out=out[P : 2 * P, :], in_=windows[1][:])
+        for m in range(2, M_TILES):
+            cols = slice((m - 2) * P, (m - 1) * P)
+            y = product(str(m), c23[:, cols], s23[:, cols], 0, S, f"y{m}")
+            scatter(windows[m % 3], y, 0, S)
+            nc.sync.dma_start(out=out[m * P : (m + 1) * P, :], in_=windows[m % 3][:])

@@ -40,11 +40,9 @@ def tile_list_tabhs_none_kernel(tc, tab, w, wgo, offs, offs2, out):
         words = keep.tile([P, T], U32, name="words", align_bytes=64)
         scales = keep.tile([P, T], U8, name="scales", align_bytes=64)
         weights_of_place = keep.tile([P, S], F32, name="weights_of_place", align_bytes=64)
-        w_raw_0 = keep.tile([P, PACK, P], F32, name="w_raw_0", align_bytes=64)
-        w_raw_1 = keep.tile([P, PACK, P], F32, name="w_raw_1", tag="raw_1", align_bytes=64)
-        w_raw_23 = keep.tile([P, PACK, 2 * P], F32, name="w_raw_23", tag="raw_23", align_bytes=64)
+        w_raw_0 = keep.tile([P, PACK, P], F32, name="w_raw_0", tag="chain_a", align_bytes=64)
 
-        nc.gpsimd.memset(scales[:].bitcast(I32), 0)
+        nc.vector.memset(scales[:].bitcast(I32), 0)
         nc.sync.dma_start(pick[:], offs)
         nc.scalar.dma_start(out=w_raw_0[:], in_=w_rows[:, :, 0:P])
         nc.sync.dma_start(place[:], offs2)
@@ -54,17 +52,15 @@ def tile_list_tabhs_none_kernel(tc, tab, w, wgo, offs, offs2, out):
                 out=scales[32 * quad : 32 * quad + 4, :].bitcast(I32),
                 in_=tab_scales[4 * quad : 4 * quad + 4, :].bitcast(I32),
             )
-        nc.sync.dma_start(out=weights_of_place[:], in_=wgo)
-        nc.sync.dma_start(out=w_raw_1[:], in_=w_rows[:, :, P : 2 * P])
-        nc.sync.dma_start(out=w_raw_23[:], in_=w_rows[:, :, 2 * P : 4 * P])
+        nc.gpsimd.dma_start(out=weights_of_place[:], in_=wgo)
         windows = []
         for i in range(3):
             window = keep.tile([P, T], F32, name=f"window{i}", align_bytes=64)
             nc.vector.memset(window[:], 0.0)
             windows.append(window)
 
-        def interleave(name, raw, width):
-            grouped = keep.tile([P, width, PACK], BF16, name=f"w_grouped{name}", align_bytes=64)
+        def interleave(name, raw, width, tag):
+            grouped = keep.tile([P, width, PACK], BF16, name=f"w_grouped{name}", tag=tag, align_bytes=64)
             nc.scalar.copy(grouped[:], raw.rearrange("p j c -> p c j"))
             return grouped
 
@@ -78,21 +74,24 @@ def tile_list_tabhs_none_kernel(tc, tab, w, wgo, offs, offs2, out):
             )
             return codes, code_scales
 
-        picked_scales = keep.tile([P, S], U8, name="picked_scales", align_bytes=64)
-        picked_words = keep.tile([P, S], U32, name="picked_words", align_bytes=64)
+        picked_scales = [keep.tile([P, HALF], U8, name=f"picked_scales{h}", align_bytes=64) for h in range(2)]
+        picked_words = [keep.tile([P, HALF], U32, name=f"picked_words{h}", align_bytes=64) for h in range(2)]
+        halves = [pick[:, h * HALF_COLS : (h + 1) * HALF_COLS] for h in range(2)]
 
-        def product(name, codes, code_scales, lo, hi, tag):
-            bank = psum.tile([P, hi - lo], F32, name=f"bank{name}")
-            nc.tensor.matmul_mx(
-                out=bank[:],
-                lhsT=codes.bitcast(FP8X4),
-                lhsT_scale=code_scales,
-                rhs=picked_words[:, lo:hi].bitcast(FP8X4),
-                rhs_scale=picked_scales[:, lo:hi],
-                start=True,
-                stop=True,
-            )
-            y = keep.tile([P, hi - lo], F32, name=f"y{name}", tag=tag, align_bytes=64)
+        def product(name, codes, code_scales, which, tag):
+            width = HALF * len(which)
+            bank = psum.tile([P, width], F32, name=f"bank{name}")
+            for i, h in enumerate(which):
+                nc.tensor.matmul_mx(
+                    out=bank[:, i * HALF : (i + 1) * HALF],
+                    lhsT=codes.bitcast(FP8X4),
+                    lhsT_scale=code_scales,
+                    rhs=picked_words[h][:].bitcast(FP8X4),
+                    rhs_scale=picked_scales[h][:],
+                    start=True,
+                    stop=True,
+                )
+            y = keep.tile([P, width], F32, name=f"y{name}", tag=tag, align_bytes=64)
             nc.scalar.copy(y[:], bank[:])
             return y
 
@@ -104,25 +103,27 @@ def tile_list_tabhs_none_kernel(tc, tab, w, wgo, offs, offs2, out):
                 mult,
             )
 
-        nc.vector.tensor_copy(picked_scales[:], scales[:].indirect(pick[:]))
-        c0, s0 = quantize("0", interleave("0", w_raw_0[:], P), P)
-        for h in range(2):
-            nc.vector.tensor_copy(
-                picked_words[:, h * HALF : (h + 1) * HALF],
-                words[:].indirect(pick[:, h * HALF_COLS : (h + 1) * HALF_COLS]),
-            )
-        y0a = product("0a", c0[:], s0[:], 0, HALF, "y0a")
+        nc.vector.tensor_copy(picked_scales[0][:], scales[:].indirect(halves[0]))
+        c0, s0 = quantize("0", interleave("0", w_raw_0[:], P, "chain_b"), P)
+        w_raw_1 = keep.tile([P, PACK, P], F32, name="w_raw_1", tag="chain_a", align_bytes=64)
+        nc.sync.dma_start(out=w_raw_1[:], in_=w_rows[:, :, P : 2 * P])
+        w_raw_23 = keep.tile([P, PACK, 2 * P], F32, name="w_raw_23", tag="chain_b", align_bytes=64)
+        nc.sync.dma_start(out=w_raw_23[:], in_=w_rows[:, :, 2 * P : 4 * P])
+        nc.vector.tensor_copy(picked_words[0][:], words[:].indirect(halves[0]))
+        nc.vector.tensor_copy(picked_scales[1][:], scales[:].indirect(halves[1]))
+        nc.vector.tensor_copy(picked_words[1][:], words[:].indirect(halves[1]))
+        y0a = product("0a", c0[:], s0[:], [0], "y0a")
         scatter(windows[0], y0a, 0, HALF)
-        c1, s1 = quantize("1", interleave("1", w_raw_1[:], P), P)
-        y0b = product("0b", c0[:], s0[:], HALF, S, "raw_1")
+        c1, s1 = quantize("1", interleave("1", w_raw_1[:], P, "grouped_1"), P)
+        y0b = product("0b", c0[:], s0[:], [1], "chain_a")
         scatter(windows[0], y0b, HALF, S)
         nc.sync.dma_start(out=out[0:P, :], in_=windows[0][:])
-        c23, s23 = quantize("23", interleave("23", w_raw_23[:], 2 * P), 2 * P)
-        y1 = product("1", c1[:], s1[:], 0, S, "raw_23")
+        c23, s23 = quantize("23", interleave("23", w_raw_23[:], 2 * P, "grouped_23"), 2 * P)
+        y1 = product("1", c1[:], s1[:], [0, 1], "chain_b")
         scatter(windows[1], y1, 0, S)
         nc.sync.dma_start(out=out[P : 2 * P, :], in_=windows[1][:])
         for m in range(2, M_TILES):
             cols = slice((m - 2) * P, (m - 1) * P)
-            y = product(str(m), c23[:, cols], s23[:, cols], 0, S, f"y{m}")
+            y = product(str(m), c23[:, cols], s23[:, cols], [0, 1], f"y{m}")
             scatter(windows[m % 3], y, 0, S)
             nc.sync.dma_start(out=out[m * P : (m + 1) * P, :], in_=windows[m % 3][:])

@@ -37,8 +37,9 @@ def tile_list_tabhs_none_kernel(tc, tab, w, wgo, offs, offs2, out):
         pick = lists.tile([P, LIST_COLS], U16, name="pick")
         place = lists.tile([P, LIST_COLS], U16, name="place")
 
+        reuse = ctx.enter_context(tc.tile_pool(name="reuse", bufs=1))
         words = keep.tile([P, T], U32, name="words", align_bytes=64)
-        scales = keep.tile([P, T], U8, name="scales", align_bytes=64)
+        scales = reuse.tile([P, T], U8, name="scales", align_bytes=64, offset=4032)
         weights_of_place = keep.tile([P, S], F32, name="weights_of_place", align_bytes=64)
         w_raw_0 = keep.tile([P, PACK, P], F32, name="w_raw_0", tag="chain_a", align_bytes=64)
 
@@ -54,7 +55,7 @@ def tile_list_tabhs_none_kernel(tc, tab, w, wgo, offs, offs2, out):
             )
         nc.gpsimd.dma_start(out=weights_of_place[:], in_=wgo)
         windows = []
-        for i in range(3):
+        for i in range(2):
             window = keep.tile([P, T], F32, name=f"window{i}", align_bytes=64)
             nc.vector.memset(window[:], 0.0)
             windows.append(window)
@@ -66,7 +67,10 @@ def tile_list_tabhs_none_kernel(tc, tab, w, wgo, offs, offs2, out):
 
         def quantize(name, grouped, width):
             codes = keep.tile([P, width], U32, name=f"w_codes{name}", align_bytes=64)
-            code_scales = keep.tile([P, width], U8, name=f"w_scales{name}", align_bytes=64)
+            if name == "0":
+                code_scales = reuse.tile([P, width], U8, name="w_scales0", align_bytes=64, offset=4096)
+            else:
+                code_scales = keep.tile([P, width], U8, name=f"w_scales{name}", align_bytes=64)
             nc.vector.quantize_mx(
                 out=codes[:].bitcast(FP8X4),
                 scales=code_scales[:],
@@ -74,24 +78,32 @@ def tile_list_tabhs_none_kernel(tc, tab, w, wgo, offs, offs2, out):
             )
             return codes, code_scales
 
-        picked_scales = [keep.tile([P, HALF], U8, name=f"picked_scales{h}", align_bytes=64) for h in range(2)]
-        picked_words = [keep.tile([P, HALF], U32, name=f"picked_words{h}", align_bytes=64) for h in range(2)]
-        halves = [pick[:, h * HALF_COLS : (h + 1) * HALF_COLS] for h in range(2)]
+        picked_scales = keep.tile([P, S], U8, name="picked_scales", align_bytes=64)
+        pieces = [(0, P), (P, HALF), (HALF, S)]
+        nc.vector.tensor_copy(picked_scales[:], scales[:].indirect(pick[:]))
+        picked_words = reuse.tile([P, S], U32, name="picked_words", align_bytes=64, offset=4096 + P)
+
+        def gather_words(i):
+            lo, hi = pieces[i]
+            nc.vector.tensor_copy(picked_words[:, lo:hi], words[:].indirect(pick[:, lo // 16 : hi // 16]))
 
         def product(name, codes, code_scales, which, tag):
-            width = HALF * len(which)
+            first = pieces[which[0]][0]
+            width = pieces[which[-1]][1] - first
             bank = psum.tile([P, width], F32, name=f"bank{name}")
-            for i, h in enumerate(which):
-                nc.tensor.matmul_mx(
-                    out=bank[:, i * HALF : (i + 1) * HALF],
-                    lhsT=codes.bitcast(FP8X4),
-                    lhsT_scale=code_scales,
-                    rhs=picked_words[h][:].bitcast(FP8X4),
-                    rhs_scale=picked_scales[h][:],
-                    start=True,
-                    stop=True,
-                )
-            y = keep.tile([P, width], F32, name=f"y{name}", tag=tag, align_bytes=64)
+            nc.tensor.matmul_mx(
+                out=bank[:],
+                lhsT=codes.bitcast(FP8X4),
+                lhsT_scale=code_scales,
+                rhs=picked_words[:, first : first + width].bitcast(FP8X4),
+                rhs_scale=picked_scales[:, first : first + width],
+                start=True,
+                stop=True,
+            )
+            if name == "1":
+                y = reuse.tile([P, width], F32, name="y1", align_bytes=64, offset=0)
+            else:
+                y = keep.tile([P, width], F32, name=f"y{name}", tag=tag, align_bytes=64)
             nc.scalar.copy(y[:], bank[:])
             return y
 
@@ -103,27 +115,27 @@ def tile_list_tabhs_none_kernel(tc, tab, w, wgo, offs, offs2, out):
                 mult,
             )
 
-        nc.vector.tensor_copy(picked_scales[0][:], scales[:].indirect(halves[0]))
-        c0, s0 = quantize("0", interleave("0", w_raw_0[:], P, "chain_b"), P)
+        c0, s0 = quantize("0", interleave("0", w_raw_0[:], P, "grouped_0"), P)
         w_raw_1 = keep.tile([P, PACK, P], F32, name="w_raw_1", tag="chain_a", align_bytes=64)
         nc.sync.dma_start(out=w_raw_1[:], in_=w_rows[:, :, P : 2 * P])
-        w_raw_23 = keep.tile([P, PACK, 2 * P], F32, name="w_raw_23", tag="chain_b", align_bytes=64)
+        w_raw_23 = reuse.tile([P, PACK, 2 * P], F32, name="w_raw_23", align_bytes=64, offset=0)
         nc.sync.dma_start(out=w_raw_23[:], in_=w_rows[:, :, 2 * P : 4 * P])
-        nc.vector.tensor_copy(picked_words[0][:], words[:].indirect(halves[0]))
-        nc.vector.tensor_copy(picked_scales[1][:], scales[:].indirect(halves[1]))
-        nc.vector.tensor_copy(picked_words[1][:], words[:].indirect(halves[1]))
-        y0a = product("0a", c0[:], s0[:], [0], "y0a")
-        scatter(windows[0], y0a, 0, HALF)
+        gather_words(0)
+        gather_words(1)
+        gather_words(2)
+        for i in range(2):
+            y = product(f"0a{i}", c0[:], s0[:], [i], f"y0a{i}")
+            scatter(windows[0], y, *pieces[i])
         c1, s1 = quantize("1", interleave("1", w_raw_1[:], P, "grouped_1"), P)
-        y0b = product("0b", c0[:], s0[:], [1], "chain_a")
+        y0b = product("0b", c0[:], s0[:], [2], "chain_a")
         scatter(windows[0], y0b, HALF, S)
         nc.sync.dma_start(out=out[0:P, :], in_=windows[0][:])
         c23, s23 = quantize("23", interleave("23", w_raw_23[:], 2 * P, "grouped_23"), 2 * P)
-        y1 = product("1", c1[:], s1[:], [0, 1], "chain_b")
+        y1 = product("1", c1[:], s1[:], [0, 1, 2], "chain_b")
         scatter(windows[1], y1, 0, S)
         nc.sync.dma_start(out=out[P : 2 * P, :], in_=windows[1][:])
         for m in range(2, M_TILES):
             cols = slice((m - 2) * P, (m - 1) * P)
-            y = product(str(m), c23[:, cols], s23[:, cols], [0, 1], f"y{m}")
-            scatter(windows[m % 3], y, 0, S)
-            nc.sync.dma_start(out=out[m * P : (m + 1) * P, :], in_=windows[m % 3][:])
+            y = product(str(m), c23[:, cols], s23[:, cols], [0, 1, 2], f"y{m}")
+            scatter(windows[m % 2], y, 0, S)
+            nc.sync.dma_start(out=out[m * P : (m + 1) * P, :], in_=windows[m % 2][:])

@@ -39,21 +39,25 @@ def tile_list_tabhs_none_kernel(tc, tab, w, wgo, offs, offs2, out):
 
         reuse = ctx.enter_context(tc.tile_pool(name="reuse", bufs=1))
         words = keep.tile([P, T], U32, name="words", align_bytes=64)
-        scales = reuse.tile([P, T], U8, name="scales", align_bytes=64, offset=4032)
+        scales = reuse.tile([P, T], U8, name="scales", align_bytes=64, offset=0)
         weights_of_place = keep.tile([P, S], F32, name="weights_of_place", align_bytes=64)
-        w_raw_0 = keep.tile([P, PACK, P], F32, name="w_raw_0", tag="chain_a", align_bytes=64)
+        w_raw_0 = keep.tile([P, PACK, P], F32, name="w_raw_0", align_bytes=64)
 
         nc.vector.memset(scales[:].bitcast(I32), 0)
         nc.sync.dma_start(pick[:], offs)
         nc.scalar.dma_start(out=w_raw_0[:], in_=w_rows[:, :, 0:P])
-        nc.sync.dma_start(place[:], offs2)
-        nc.scalar.dma_start(out=words[:].bitcast(I32), in_=tab_words.bitcast(I32))
         for quad in range(4):
             nc.sync.dma_start(
                 out=scales[32 * quad : 32 * quad + 4, :].bitcast(I32),
                 in_=tab_scales[4 * quad : 4 * quad + 4, :].bitcast(I32),
             )
-        nc.gpsimd.dma_start(out=weights_of_place[:], in_=wgo)
+        nc.sync.dma_start(out=words[:].bitcast(I32), in_=tab_words.bitcast(I32))
+        nc.sync.dma_start(place[:], offs2)
+        nc.sync.dma_start(out=weights_of_place[:], in_=wgo)
+        w_raw_1 = keep.tile([P, PACK, P], F32, name="w_raw_1", tag="chain_a", align_bytes=64)
+        nc.sync.dma_start(out=w_raw_1[:], in_=w_rows[:, :, P : 2 * P])
+        w_raw_23 = keep.tile([P, PACK, 2 * P], F32, name="w_raw_23", tag="chain_b", align_bytes=64)
+        nc.sync.dma_start(out=w_raw_23[:], in_=w_rows[:, :, 2 * P : 4 * P])
         windows = []
         for i in range(2):
             window = keep.tile([P, T], F32, name=f"window{i}", align_bytes=64)
@@ -68,7 +72,7 @@ def tile_list_tabhs_none_kernel(tc, tab, w, wgo, offs, offs2, out):
         def quantize(name, grouped, width):
             codes = keep.tile([P, width], U32, name=f"w_codes{name}", align_bytes=64)
             if name == "0":
-                code_scales = reuse.tile([P, width], U8, name="w_scales0", align_bytes=64, offset=4096)
+                code_scales = reuse.tile([P, width], U8, name="w_scales0", align_bytes=64, offset=0)
             else:
                 code_scales = keep.tile([P, width], U8, name=f"w_scales{name}", align_bytes=64)
             nc.vector.quantize_mx(
@@ -81,7 +85,7 @@ def tile_list_tabhs_none_kernel(tc, tab, w, wgo, offs, offs2, out):
         picked_scales = keep.tile([P, S], U8, name="picked_scales", align_bytes=64)
         pieces = [(0, P), (P, HALF), (HALF, S)]
         nc.vector.tensor_copy(picked_scales[:], scales[:].indirect(pick[:]))
-        picked_words = reuse.tile([P, S], U32, name="picked_words", align_bytes=64, offset=4096 + P)
+        picked_words = reuse.tile([P, S], U32, name="picked_words", align_bytes=64, offset=P)
 
         def gather_words(i):
             lo, hi = pieces[i]
@@ -100,10 +104,7 @@ def tile_list_tabhs_none_kernel(tc, tab, w, wgo, offs, offs2, out):
                 start=True,
                 stop=True,
             )
-            if name == "1":
-                y = reuse.tile([P, width], F32, name="y1", align_bytes=64, offset=0)
-            else:
-                y = keep.tile([P, width], F32, name=f"y{name}", tag=tag, align_bytes=64)
+            y = keep.tile([P, width], F32, name=f"y{name}", tag=tag, align_bytes=64)
             nc.scalar.copy(y[:], bank[:])
             return y
 
@@ -116,10 +117,6 @@ def tile_list_tabhs_none_kernel(tc, tab, w, wgo, offs, offs2, out):
             )
 
         c0, s0 = quantize("0", interleave("0", w_raw_0[:], P, "grouped_0"), P)
-        w_raw_1 = keep.tile([P, PACK, P], F32, name="w_raw_1", tag="chain_a", align_bytes=64)
-        nc.sync.dma_start(out=w_raw_1[:], in_=w_rows[:, :, P : 2 * P])
-        w_raw_23 = reuse.tile([P, PACK, 2 * P], F32, name="w_raw_23", align_bytes=64, offset=0)
-        nc.sync.dma_start(out=w_raw_23[:], in_=w_rows[:, :, 2 * P : 4 * P])
         gather_words(0)
         gather_words(1)
         gather_words(2)

@@ -37,9 +37,8 @@ def tile_list_tabhs_none_kernel(tc, tab, w, wgo, offs, offs2, out):
         pick = lists.tile([P, LIST_COLS], U16, name="pick")
         place = lists.tile([P, LIST_COLS], U16, name="place")
 
-        reuse = ctx.enter_context(tc.tile_pool(name="reuse", bufs=1))
         words = keep.tile([P, T], U32, name="words", align_bytes=64)
-        scales = reuse.tile([P, T], U8, name="scales", align_bytes=64, offset=0)
+        scales = keep.tile([P, T], U8, name="scales", align_bytes=64)
         weights_of_place = keep.tile([P, S], F32, name="weights_of_place", align_bytes=64)
         w_raw_0 = keep.tile([P, PACK, P], F32, name="w_raw_0", align_bytes=64)
 
@@ -71,10 +70,7 @@ def tile_list_tabhs_none_kernel(tc, tab, w, wgo, offs, offs2, out):
 
         def quantize(name, grouped, width):
             codes = keep.tile([P, width], U32, name=f"w_codes{name}", align_bytes=64)
-            if name == "0":
-                code_scales = reuse.tile([P, width], U8, name="w_scales0", align_bytes=64, offset=0)
-            else:
-                code_scales = keep.tile([P, width], U8, name=f"w_scales{name}", align_bytes=64)
+            code_scales = keep.tile([P, width], U8, name=f"w_scales{name}", align_bytes=64)
             nc.vector.quantize_mx(
                 out=codes[:].bitcast(FP8X4),
                 scales=code_scales[:],
@@ -85,7 +81,7 @@ def tile_list_tabhs_none_kernel(tc, tab, w, wgo, offs, offs2, out):
         picked_scales = keep.tile([P, S], U8, name="picked_scales", align_bytes=64)
         pieces = [(0, P), (P, HALF), (HALF, S)]
         nc.vector.tensor_copy(picked_scales[:], scales[:].indirect(pick[:]))
-        picked_words = reuse.tile([P, S], U32, name="picked_words", align_bytes=64, offset=P)
+        picked_words = keep.tile([P, S], U32, name="picked_words", align_bytes=64)
 
         def gather_words(i):
             lo, hi = pieces[i]

@@ -46,7 +46,8 @@ def tile_list_tabhs_none_kernel(tc, tab, w, wgo, offs, offs2, out):
         nc.sync.dma_start(pick[:], offs)
         nc.scalar.dma_start(out=w_raw_0[:], in_=w_rows[:, :, 0:P])
         for quad in range(4):
-            nc.sync.dma_start(
+            queue = nc.sync if quad < 3 else nc.scalar
+            queue.dma_start(
                 out=scales[32 * quad : 32 * quad + 4, :].bitcast(I32),
                 in_=tab_scales[4 * quad : 4 * quad + 4, :].bitcast(I32),
             )
@@ -65,7 +66,10 @@ def tile_list_tabhs_none_kernel(tc, tab, w, wgo, offs, offs2, out):
 
         def interleave(name, raw, width, tag):
             grouped = keep.tile([P, width, PACK], BF16, name=f"w_grouped{name}", tag=tag, align_bytes=64)
-            nc.scalar.copy(grouped[:], raw.rearrange("p j c -> p c j"))
+            nc.scalar.copy(
+                grouped[:].rearrange("p (c i) j -> p c j i", i=PACK),
+                raw.rearrange("p j (c i) -> p c j i", i=PACK),
+            )
             return grouped
 
         def quantize(name, grouped, width):
@@ -83,8 +87,7 @@ def tile_list_tabhs_none_kernel(tc, tab, w, wgo, offs, offs2, out):
         nc.vector.tensor_copy(picked_scales[:], scales[:].indirect(pick[:]))
         picked_words = keep.tile([P, S], U32, name="picked_words", align_bytes=64)
 
-        def gather_words(i):
-            lo, hi = pieces[i]
+        def gather_words(lo, hi):
             nc.vector.tensor_copy(picked_words[:, lo:hi], words[:].indirect(pick[:, lo // 16 : hi // 16]))
 
         def product(name, codes, code_scales, which, tag):
@@ -113,9 +116,8 @@ def tile_list_tabhs_none_kernel(tc, tab, w, wgo, offs, offs2, out):
             )
 
         c0, s0 = quantize("0", interleave("0", w_raw_0[:], P, "grouped_0"), P)
-        gather_words(0)
-        gather_words(1)
-        gather_words(2)
+        gather_words(0, P)
+        gather_words(P, S)
         for i in range(2):
             y = product(f"0a{i}", c0[:], s0[:], [i], f"y0a{i}")
             scatter(windows[0], y, *pieces[i])

@@ -52,12 +52,15 @@ def tile_list_tabhs_none_kernel(tc, tab, w, wgo, offs, offs2, out):
                 in_=tab_scales[4 * quad : 4 * quad + 4, :].bitcast(I32),
             )
         nc.sync.dma_start(out=words[:].bitcast(I32), in_=tab_words.bitcast(I32))
-        nc.sync.dma_start(place[:], offs2)
-        nc.sync.dma_start(out=weights_of_place[:], in_=wgo)
-        w_raw_1 = keep.tile([P, PACK, P], F32, name="w_raw_1", tag="chain_a", align_bytes=64)
-        nc.sync.dma_start(out=w_raw_1[:], in_=w_rows[:, :, P : 2 * P])
-        w_raw_23 = keep.tile([P, PACK, 2 * P], F32, name="w_raw_23", tag="chain_b", align_bytes=64)
-        nc.sync.dma_start(out=w_raw_23[:], in_=w_rows[:, :, 2 * P : 4 * P])
+        nc.sync.dma_start(out=weights_of_place[:, 0:P], in_=wgo[:, 0:P])
+        w_raw = [w_raw_0]
+        for m in range(1, M_TILES):
+            raw = keep.tile([P, PACK, P], F32, name=f"w_raw_{m}", tag=f"chain_{m}", align_bytes=64)
+            nc.sync.dma_start(out=raw[:], in_=w_rows[:, :, m * P : (m + 1) * P])
+            w_raw.append(raw)
+            if m == 1:
+                nc.sync.dma_start(place[:], offs2)
+                nc.sync.dma_start(out=weights_of_place[:, P:S], in_=wgo[:, P:S])
         windows = []
         for i in range(2):
             window = keep.tile([P, T], F32, name=f"window{i}", align_bytes=64)
@@ -83,27 +86,25 @@ def tile_list_tabhs_none_kernel(tc, tab, w, wgo, offs, offs2, out):
             return codes, code_scales
 
         picked_scales = keep.tile([P, S], U8, name="picked_scales", align_bytes=64)
-        pieces = [(0, P), (P, HALF), (HALF, S)]
         nc.vector.tensor_copy(picked_scales[:], scales[:].indirect(pick[:]))
         picked_words = keep.tile([P, S], U32, name="picked_words", align_bytes=64)
 
         def gather_words(lo, hi):
             nc.vector.tensor_copy(picked_words[:, lo:hi], words[:].indirect(pick[:, lo // 16 : hi // 16]))
 
-        def product(name, codes, code_scales, which, tag):
-            first = pieces[which[0]][0]
-            width = pieces[which[-1]][1] - first
-            bank = psum.tile([P, width], F32, name=f"bank{name}")
+        def product(name, quantized, lo, hi, bank_tag, tag):
+            codes, code_scales = quantized
+            bank = psum.tile([P, hi - lo], F32, name=f"bank{name}", tag=bank_tag)
             nc.tensor.matmul_mx(
                 out=bank[:],
-                lhsT=codes.bitcast(FP8X4),
-                lhsT_scale=code_scales,
-                rhs=picked_words[:, first : first + width].bitcast(FP8X4),
-                rhs_scale=picked_scales[:, first : first + width],
+                lhsT=codes[:].bitcast(FP8X4),
+                lhsT_scale=code_scales[:],
+                rhs=picked_words[:, lo:hi].bitcast(FP8X4),
+                rhs_scale=picked_scales[:, lo:hi],
                 start=True,
                 stop=True,
             )
-            y = keep.tile([P, width], F32, name=f"y{name}", tag=tag, align_bytes=64)
+            y = keep.tile([P, hi - lo], F32, name=f"y{name}", tag=tag, align_bytes=64)
             nc.scalar.copy(y[:], bank[:])
             return y
 
@@ -115,22 +116,27 @@ def tile_list_tabhs_none_kernel(tc, tab, w, wgo, offs, offs2, out):
                 mult,
             )
 
-        c0, s0 = quantize("0", interleave("0", w_raw_0[:], P, "grouped_0"), P)
+        def weights(m):
+            return quantize(str(m), interleave(str(m), w_raw[m][:], P, f"grouped_{m}"), P)
+
+        def store(m, window):
+            nc.sync.dma_start(out=out[m * P : (m + 1) * P, :], in_=window[:])
+
+        q0 = weights(0)
         gather_words(0, P)
         gather_words(P, S)
-        for i in range(2):
-            y = product(f"0a{i}", c0[:], s0[:], [i], f"y0a{i}")
-            scatter(windows[0], y, *pieces[i])
-        c1, s1 = quantize("1", interleave("1", w_raw_1[:], P, "grouped_1"), P)
-        y0b = product("0b", c0[:], s0[:], [2], "chain_a")
-        scatter(windows[0], y0b, HALF, S)
-        nc.sync.dma_start(out=out[0:P, :], in_=windows[0][:])
-        c23, s23 = quantize("23", interleave("23", w_raw_23[:], 2 * P, "grouped_23"), 2 * P)
-        y1 = product("1", c1[:], s1[:], [0, 1, 2], "chain_b")
-        scatter(windows[1], y1, 0, S)
-        nc.sync.dma_start(out=out[P : 2 * P, :], in_=windows[1][:])
-        for m in range(2, M_TILES):
-            cols = slice((m - 2) * P, (m - 1) * P)
-            y = product(str(m), c23[:, cols], s23[:, cols], [0, 1, 2], f"y{m}")
-            scatter(windows[m % 2], y, 0, S)
-            nc.sync.dma_start(out=out[m * P : (m + 1) * P, :], in_=windows[m % 2][:])
+        scatter(windows[0], product("0a", q0, 0, P, "bank_a", "y0a"), 0, P)
+        q1 = weights(1)
+        scatter(windows[0], product("0b", q0, P, 3 * P, "bank_b", "chain_1"), P, 3 * P)
+        q2 = weights(2)
+        third = keep.tile([P, T], F32, name="window2", tag="grouped_2", align_bytes=64)
+        nc.gpsimd.memset(third[:], 0.0)
+        scatter(windows[1], product("1", q1, 0, S, "bank_c", "chain_2"), 0, S)
+        store(1, windows[1])
+        q3 = weights(3)
+        scatter(windows[0], product("0c", q0, 3 * P, S, "bank_c", "y0c"), 3 * P, S)
+        store(0, windows[0])
+        scatter(third, product("2", q2, 0, S, "bank_d", "chain_3"), 0, S)
+        store(2, third)
+        scatter(windows[1], product("3", q3, 0, S, "bank_e", "y3"), 0, S)
+        store(3, windows[1])

@@ -53,14 +53,12 @@ def tile_list_tabhs_none_kernel(tc, tab, w, wgo, offs, offs2, out):
             )
         nc.sync.dma_start(out=words[:].bitcast(I32), in_=tab_words.bitcast(I32))
         nc.sync.dma_start(out=weights_of_place[:, 0:P], in_=wgo[:, 0:P])
-        w_raw = [w_raw_0]
-        for m in range(1, M_TILES):
-            raw = keep.tile([P, PACK, P], F32, name=f"w_raw_{m}", tag=f"chain_{m}", align_bytes=64)
-            nc.sync.dma_start(out=raw[:], in_=w_rows[:, :, m * P : (m + 1) * P])
-            w_raw.append(raw)
-            if m == 1:
-                nc.sync.dma_start(place[:], offs2)
-                nc.sync.dma_start(out=weights_of_place[:, P:S], in_=wgo[:, P:S])
+        w_raw_1 = keep.tile([P, PACK, P], F32, name="w_raw_1", tag="chain_a", align_bytes=64)
+        nc.sync.dma_start(out=w_raw_1[:], in_=w_rows[:, :, P : 2 * P])
+        nc.sync.dma_start(place[:], offs2)
+        nc.sync.dma_start(out=weights_of_place[:, P:S], in_=wgo[:, P:S])
+        w_raw_23 = keep.tile([P, PACK, 2 * P], F32, name="w_raw_23", tag="chain_b", align_bytes=64)
+        nc.sync.dma_start(out=w_raw_23[:], in_=w_rows[:, :, 2 * P : 4 * P])
         windows = []
         for i in range(2):
             window = keep.tile([P, T], F32, name=f"window{i}", align_bytes=64)
@@ -75,15 +73,15 @@ def tile_list_tabhs_none_kernel(tc, tab, w, wgo, offs, offs2, out):
             )
             return grouped
 
-        def quantize(name, grouped, width):
-            codes = keep.tile([P, width], U32, name=f"w_codes{name}", align_bytes=64)
+        def quantize(name, grouped, width, tag):
+            codes = keep.tile([P, width], U32, name=f"w_codes{name}", tag=tag, align_bytes=64)
             code_scales = keep.tile([P, width], U8, name=f"w_scales{name}", align_bytes=64)
             nc.vector.quantize_mx(
                 out=codes[:].bitcast(FP8X4),
                 scales=code_scales[:],
                 in_=grouped[:].rearrange("p c j -> p (c j)"),
             )
-            return codes, code_scales
+            return codes[:], code_scales[:]
 
         picked_scales = keep.tile([P, S], U8, name="picked_scales", align_bytes=64)
         nc.vector.tensor_copy(picked_scales[:], scales[:].indirect(pick[:]))
@@ -92,51 +90,58 @@ def tile_list_tabhs_none_kernel(tc, tab, w, wgo, offs, offs2, out):
         def gather_words(lo, hi):
             nc.vector.tensor_copy(picked_words[:, lo:hi], words[:].indirect(pick[:, lo // 16 : hi // 16]))
 
-        def product(name, quantized, lo, hi, bank_tag, tag):
+        def product(name, quantized, lo, hi):
             codes, code_scales = quantized
-            bank = psum.tile([P, hi - lo], F32, name=f"bank{name}", tag=bank_tag)
+            bank = psum.tile([P, hi - lo], F32, name=f"bank{name}")
             nc.tensor.matmul_mx(
                 out=bank[:],
-                lhsT=codes[:].bitcast(FP8X4),
-                lhsT_scale=code_scales[:],
+                lhsT=codes.bitcast(FP8X4),
+                lhsT_scale=code_scales,
                 rhs=picked_words[:, lo:hi].bitcast(FP8X4),
                 rhs_scale=picked_scales[:, lo:hi],
                 start=True,
                 stop=True,
             )
-            y = keep.tile([P, hi - lo], F32, name=f"y{name}", tag=tag, align_bytes=64)
-            nc.scalar.copy(y[:], bank[:])
-            return y
+            return bank
+
+        def result(name, width, tag):
+            return keep.tile([P, width], F32, name=f"y{name}", tag=tag, align_bytes=64)
+
+        def drained(name, bank, width, tag):
+            y = result(name, width, tag)
+            nc.scalar.copy(y[:], bank)
+            return y[:]
 
         def scatter(window, y, lo, hi):
             nc.vector.tensor_tensor(
                 window[:].indirect(place[:, lo // 16 : hi // 16]),
-                y[:],
+                y,
                 weights_of_place[:, lo:hi],
                 mult,
             )
 
-        def weights(m):
-            return quantize(str(m), interleave(str(m), w_raw[m][:], P, f"grouped_{m}"), P)
-
         def store(m, window):
             nc.sync.dma_start(out=out[m * P : (m + 1) * P, :], in_=window[:])
 
-        q0 = weights(0)
+        q0 = quantize("0", interleave("0", w_raw_0[:], P, "grouped_0"), P, "codes_0")
         gather_words(0, P)
         gather_words(P, S)
-        scatter(windows[0], product("0a", q0, 0, P, "bank_a", "y0a"), 0, P)
-        q1 = weights(1)
-        scatter(windows[0], product("0b", q0, P, 3 * P, "bank_b", "chain_1"), P, 3 * P)
-        q2 = weights(2)
-        third = keep.tile([P, T], F32, name="window2", tag="grouped_2", align_bytes=64)
+        scatter(windows[0], drained("0a", product("0a", q0, 0, P)[:], P, "y0a"), 0, P)
+        q1 = quantize("1", interleave("1", w_raw_1[:], P, "grouped_1"), P, "chain_c")
+        scatter(windows[0], drained("0b", product("0b", q0, P, 3 * P)[:], HALF, "chain_a"), P, 3 * P)
+        bank_1 = product("1", q1, 0, S)
+        scatter(windows[1], drained("1a", bank_1[:, 0:HALF], HALF, "y1a"), 0, HALF)
+        c23, s23 = quantize("23", interleave("23", w_raw_23[:], 2 * P, "chain_c"), 2 * P, "codes_23")
+        third = keep.tile([P, T], F32, name="window2", tag="chain_c", align_bytes=64)
         nc.gpsimd.memset(third[:], 0.0)
-        scatter(windows[1], product("1", q1, 0, S, "bank_c", "chain_2"), 0, S)
-        store(1, windows[1])
-        q3 = weights(3)
-        scatter(windows[0], product("0c", q0, 3 * P, S, "bank_c", "y0c"), 3 * P, S)
+        late = result("late", 3 * P, "chain_b")
+        nc.scalar.copy(late[:, 0:P], product("0c", q0, 3 * P, S)[:])
+        scatter(windows[0], late[:, 0:P], 3 * P, S)
         store(0, windows[0])
-        scatter(third, product("2", q2, 0, S, "bank_d", "chain_3"), 0, S)
+        nc.scalar.copy(late[:, P : 3 * P], bank_1[:, HALF:S])
+        scatter(windows[1], late[:, P : 3 * P], HALF, S)
+        store(1, windows[1])
+        scatter(third, drained("2", product("2", (c23[:, 0:P], s23[:, 0:P]), 0, S)[:], S, "y2"), 0, S)
         store(2, third)
-        scatter(windows[1], product("3", q3, 0, S, "bank_e", "y3"), 0, S)
-        store(3, windows[1])
+        scatter(windows[0], drained("3", product("3", (c23[:, P : 2 * P], s23[:, P : 2 * P]), 0, S)[:], S, "y3"), 0, S)
+        store(3, windows[0])

@@ -52,9 +52,9 @@ def tile_list_tabhs_none_kernel(tc, tab, w, wgo, offs, offs2, out):
                 in_=tab_scales[4 * quad : 4 * quad + 4, :].bitcast(I32),
             )
         nc.sync.dma_start(out=words[:].bitcast(I32), in_=tab_words.bitcast(I32))
-        nc.sync.dma_start(out=weights_of_place[:, 0:P], in_=wgo[:, 0:P])
         w_raw_1 = keep.tile([P, PACK, P], F32, name="w_raw_1", tag="chain_a", align_bytes=64)
         nc.sync.dma_start(out=w_raw_1[:], in_=w_rows[:, :, P : 2 * P])
+        nc.gpsimd.dma_start(out=weights_of_place[:, 0:P], in_=wgo[:, 0:P])
         nc.sync.dma_start(place[:], offs2)
         nc.sync.dma_start(out=weights_of_place[:, P:S], in_=wgo[:, P:S])
         w_raw_23 = keep.tile([P, PACK, 2 * P], F32, name="w_raw_23", tag="chain_b", align_bytes=64)

@@ -60,7 +60,7 @@ def tile_list_tabhs_none_kernel(tc, tab, w, wgo, offs, offs2, out):
         w_raw_23 = keep.tile([P, PACK, 2 * P], F32, name="w_raw_23", tag="chain_b", align_bytes=64)
         nc.sync.dma_start(out=w_raw_23[:], in_=w_rows[:, :, 2 * P : 4 * P])
         windows = []
-        for i in range(2):
+        for i in range(3):
             window = keep.tile([P, T], F32, name=f"window{i}", align_bytes=64)
             nc.vector.memset(window[:], 0.0)
             windows.append(window)
@@ -132,8 +132,6 @@ def tile_list_tabhs_none_kernel(tc, tab, w, wgo, offs, offs2, out):
         bank_1 = product("1", q1, 0, S)
         scatter(windows[1], drained("1a", bank_1[:, 0:HALF], HALF, "y1a"), 0, HALF)
         c23, s23 = quantize("23", interleave("23", w_raw_23[:], 2 * P, "chain_c"), 2 * P, "codes_23")
-        third = keep.tile([P, T], F32, name="window2", tag="chain_c", align_bytes=64)
-        nc.gpsimd.memset(third[:], 0.0)
         late = result("late", 3 * P, "chain_b")
         nc.scalar.copy(late[:, 0:P], product("0c", q0, 3 * P, S)[:])
         scatter(windows[0], late[:, 0:P], 3 * P, S)
@@ -141,7 +139,7 @@ def tile_list_tabhs_none_kernel(tc, tab, w, wgo, offs, offs2, out):
         nc.scalar.copy(late[:, P : 3 * P], bank_1[:, HALF:S])
         scatter(windows[1], late[:, P : 3 * P], HALF, S)
         store(1, windows[1])
-        scatter(third, drained("2", product("2", (c23[:, 0:P], s23[:, 0:P]), 0, S)[:], S, "y2"), 0, S)
-        store(2, third)
+        scatter(windows[2], drained("2", product("2", (c23[:, 0:P], s23[:, 0:P]), 0, S)[:], S, "y2"), 0, S)
+        store(2, windows[2])
         scatter(windows[0], drained("3", product("3", (c23[:, P : 2 * P], s23[:, P : 2 * P]), 0, S)[:], S, "y3"), 0, S)
         store(3, windows[0])

@@ -32,6 +32,7 @@ def tile_list_tabhs_none_kernel(tc, tab, w, wgo, offs, offs2, out):
     with ExitStack() as ctx:
         lists = ctx.enter_context(tc.tile_pool(name="lists", bufs=1))
         keep = ctx.enter_context(tc.tile_pool(name="keep", bufs=1))
+        turns = ctx.enter_context(tc.tile_pool(name="turns", bufs=1))
         psum = ctx.enter_context(tc.psum_pool(name="psum", bufs=1))
 
         pick = lists.tile([P, LIST_COLS], U16, name="pick")
@@ -52,7 +53,7 @@ def tile_list_tabhs_none_kernel(tc, tab, w, wgo, offs, offs2, out):
                 in_=tab_scales[4 * quad : 4 * quad + 4, :].bitcast(I32),
             )
         nc.sync.dma_start(out=words[:].bitcast(I32), in_=tab_words.bitcast(I32))
-        w_raw_1 = keep.tile([P, PACK, P], F32, name="w_raw_1", tag="chain_a", align_bytes=64)
+        w_raw_1 = turns.tile([P, PACK, P], F32, name="w_raw_1", offset=0, align_bytes=64)
         nc.sync.dma_start(out=w_raw_1[:], in_=w_rows[:, :, P : 2 * P])
         nc.gpsimd.dma_start(out=weights_of_place[:, 0:P], in_=wgo[:, 0:P])
         nc.sync.dma_start(place[:], offs2)
@@ -83,8 +84,9 @@ def tile_list_tabhs_none_kernel(tc, tab, w, wgo, offs, offs2, out):
             )
             return codes[:], code_scales[:]
 
-        picked_scales = keep.tile([P, S], U8, name="picked_scales", align_bytes=64)
-        nc.vector.tensor_copy(picked_scales[:], scales[:].indirect(pick[:]))
+        picked_scales = keep.tile([P, 3 * P], U8, name="picked_scales", align_bytes=64)
+        nc.vector.tensor_copy(picked_scales[:], scales[:].indirect(pick[:, 0 : 3 * P // 16]))
+        late_scales = turns.tile([P, P], U8, name="late_scales", offset=4 * HALF, align_bytes=64)
         picked_words = keep.tile([P, S], U32, name="picked_words", align_bytes=64)
 
         def gather_words(lo, hi):
@@ -93,15 +95,18 @@ def tile_list_tabhs_none_kernel(tc, tab, w, wgo, offs, offs2, out):
         def product(name, quantized, lo, hi):
             codes, code_scales = quantized
             bank = psum.tile([P, hi - lo], F32, name=f"bank{name}")
-            nc.tensor.matmul_mx(
-                out=bank[:],
-                lhsT=codes.bitcast(FP8X4),
-                lhsT_scale=code_scales,
-                rhs=picked_words[:, lo:hi].bitcast(FP8X4),
-                rhs_scale=picked_scales[:, lo:hi],
-                start=True,
-                stop=True,
-            )
+            for a, b, plane in ((0, P, picked_scales), (P, 3 * P, picked_scales), (3 * P, S, late_scales)) if lo != HALF and hi != HALF else (
+                (0, HALF, picked_scales), (HALF, 3 * P, picked_scales), (3 * P, S, late_scales)):
+                if a >= lo and b <= hi:
+                    nc.tensor.matmul_mx(
+                        out=bank[:, a - lo : b - lo],
+                        lhsT=codes.bitcast(FP8X4),
+                        lhsT_scale=code_scales,
+                        rhs=picked_words[:, a:b].bitcast(FP8X4),
+                        rhs_scale=plane[:, a:b] if a < 3 * P else plane[:],
+                        start=True,
+                        stop=True,
+                    )
             return bank
 
         def result(name, width, tag):
@@ -128,15 +133,17 @@ def tile_list_tabhs_none_kernel(tc, tab, w, wgo, offs, offs2, out):
         gather_words(P, S)
         scatter(windows[0], drained("0a", product("0a", q0, 0, P)[:], P, "y0a"), 0, P)
         q1 = quantize("1", interleave("1", w_raw_1[:], P, "grouped_1"), P, "chain_c")
-        scatter(windows[0], drained("0b", product("0b", q0, P, 3 * P)[:], HALF, "chain_a"), P, 3 * P)
-        bank_1 = product("1", q1, 0, S)
-        scatter(windows[1], drained("1a", bank_1[:, 0:HALF], HALF, "y1a"), 0, HALF)
+        nc.vector.tensor_copy(late_scales[:], scales[:].indirect(pick[:, 3 * P // 16 : S // 16]))
+        y0b = turns.tile([P, HALF], F32, name="y0b", offset=0, align_bytes=64)
+        nc.scalar.copy(y0b[:], product("0b", q0, P, 3 * P)[:])
+        scatter(windows[0], y0b[:], P, 3 * P)
+        scatter(windows[1], drained("1a", product("1a", q1, 0, HALF)[:], HALF, "y1a"), 0, HALF)
         c23, s23 = quantize("23", interleave("23", w_raw_23[:], 2 * P, "chain_c"), 2 * P, "codes_23")
         late = result("late", 3 * P, "chain_b")
         nc.scalar.copy(late[:, 0:P], product("0c", q0, 3 * P, S)[:])
         scatter(windows[0], late[:, 0:P], 3 * P, S)
         store(0, windows[0])
-        nc.scalar.copy(late[:, P : 3 * P], bank_1[:, HALF:S])
+        nc.scalar.copy(late[:, P : 3 * P], product("1b", q1, HALF, S)[:])
         scatter(windows[1], late[:, P : 3 * P], HALF, S)
         store(1, windows[1])
         scatter(windows[2], drained("2", product("2", (c23[:, 0:P], s23[:, 0:P]), 0, S)[:], S, "y2"), 0, S)

@@ -44,8 +44,8 @@ def tile_list_tabhs_none_kernel(tc, tab, w, wgo, offs, offs2, out):
         w_raw_0 = keep.tile([P, PACK, P], F32, name="w_raw_0", align_bytes=64)
 
         nc.vector.memset(scales[:].bitcast(I32), 0)
+        nc.sync.dma_start(out=w_raw_0[:], in_=w_rows[:, :, 0:P])
         nc.sync.dma_start(pick[:], offs)
-        nc.scalar.dma_start(out=w_raw_0[:], in_=w_rows[:, :, 0:P])
         for quad in range(4):
             queue = nc.sync if quad < 3 else nc.scalar
             queue.dma_start(

@@ -41,10 +41,11 @@ def tile_list_tabhs_none_kernel(tc, tab, w, wgo, offs, offs2, out):
         words = keep.tile([P, T], U32, name="words", align_bytes=64)
         scales = keep.tile([P, T], U8, name="scales", align_bytes=64)
         weights_of_place = keep.tile([P, S], F32, name="weights_of_place", align_bytes=64)
-        w_raw_0 = keep.tile([P, PACK, P], F32, name="w_raw_0", align_bytes=64)
+        w_raw_0a = keep.tile([P, 2, P], F32, name="w_raw_0a", align_bytes=64)
+        w_raw_0b = keep.tile([P, 2, P], F32, name="w_raw_0b", align_bytes=64)
 
         nc.vector.memset(scales[:].bitcast(I32), 0)
-        nc.sync.dma_start(out=w_raw_0[:], in_=w_rows[:, :, 0:P])
+        nc.sync.dma_start(out=w_raw_0a[:], in_=w_rows[:, 0:2, 0:P])
         nc.sync.dma_start(pick[:], offs)
         for quad in range(4):
             queue = nc.sync if quad < 3 else nc.scalar
@@ -52,6 +53,7 @@ def tile_list_tabhs_none_kernel(tc, tab, w, wgo, offs, offs2, out):
                 out=scales[32 * quad : 32 * quad + 4, :].bitcast(I32),
                 in_=tab_scales[4 * quad : 4 * quad + 4, :].bitcast(I32),
             )
+        nc.sync.dma_start(out=w_raw_0b[:], in_=w_rows[:, 2:4, 0:P])
         nc.sync.dma_start(out=words[:].bitcast(I32), in_=tab_words.bitcast(I32))
         w_raw_1 = turns.tile([P, PACK, P], F32, name="w_raw_1", offset=0, align_bytes=64)
         nc.sync.dma_start(out=w_raw_1[:], in_=w_rows[:, :, P : 2 * P])
@@ -84,9 +86,7 @@ def tile_list_tabhs_none_kernel(tc, tab, w, wgo, offs, offs2, out):
             )
             return codes[:], code_scales[:]
 
-        picked_scales = keep.tile([P, 3 * P], U8, name="picked_scales", align_bytes=64)
-        nc.vector.tensor_copy(picked_scales[:], scales[:].indirect(pick[:, 0 : 3 * P // 16]))
-        late_scales = turns.tile([P, P], U8, name="late_scales", offset=4 * HALF, align_bytes=64)
+        picked_scales = keep.tile([P, S], U8, name="picked_scales", align_bytes=64)
         picked_words = keep.tile([P, S], U32, name="picked_words", align_bytes=64)
 
         def gather_words(lo, hi):
@@ -95,18 +95,15 @@ def tile_list_tabhs_none_kernel(tc, tab, w, wgo, offs, offs2, out):
         def product(name, quantized, lo, hi):
             codes, code_scales = quantized
             bank = psum.tile([P, hi - lo], F32, name=f"bank{name}")
-            for a, b, plane in ((0, P, picked_scales), (P, 3 * P, picked_scales), (3 * P, S, late_scales)) if lo != HALF and hi != HALF else (
-                (0, HALF, picked_scales), (HALF, 3 * P, picked_scales), (3 * P, S, late_scales)):
-                if a >= lo and b <= hi:
-                    nc.tensor.matmul_mx(
-                        out=bank[:, a - lo : b - lo],
-                        lhsT=codes.bitcast(FP8X4),
-                        lhsT_scale=code_scales,
-                        rhs=picked_words[:, a:b].bitcast(FP8X4),
-                        rhs_scale=plane[:, a:b] if a < 3 * P else plane[:],
-                        start=True,
-                        stop=True,
-                    )
+            nc.tensor.matmul_mx(
+                out=bank[:],
+                lhsT=codes.bitcast(FP8X4),
+                lhsT_scale=code_scales,
+                rhs=picked_words[:, lo:hi].bitcast(FP8X4),
+                rhs_scale=picked_scales[:, lo:hi],
+                start=True,
+                stop=True,
+            )
             return bank
 
         def result(name, width, tag):
@@ -128,12 +125,18 @@ def tile_list_tabhs_none_kernel(tc, tab, w, wgo, offs, offs2, out):
         def store(m, window):
             nc.sync.dma_start(out=out[m * P : (m + 1) * P, :], in_=window[:])
 
-        q0 = quantize("0", interleave("0", w_raw_0[:], P, "grouped_0"), P, "codes_0")
+        nc.vector.tensor_copy(picked_scales[:], scales[:].indirect(pick[:]))
+        grouped_0 = keep.tile([P, P, PACK], BF16, name="w_grouped0", align_bytes=64)
+        for half, raw in enumerate((w_raw_0a, w_raw_0b)):
+            nc.scalar.copy(
+                grouped_0[:, :, 2 * half : 2 * half + 2].rearrange("p (c i) j -> p c j i", i=PACK),
+                raw[:].rearrange("p j (c i) -> p c j i", i=PACK),
+            )
+        q0 = quantize("0", grouped_0, P, "codes_0")
         gather_words(0, P)
         gather_words(P, S)
         scatter(windows[0], drained("0a", product("0a", q0, 0, P)[:], P, "y0a"), 0, P)
         q1 = quantize("1", interleave("1", w_raw_1[:], P, "grouped_1"), P, "chain_c")
-        nc.vector.tensor_copy(late_scales[:], scales[:].indirect(pick[:, 3 * P // 16 : S // 16]))
         y0b = turns.tile([P, HALF], F32, name="y0b", offset=0, align_bytes=64)
         nc.scalar.copy(y0b[:], product("0b", q0, P, 3 * P)[:])
         scatter(windows[0], y0b[:], P, 3 * P)

@@ -15,10 +15,7 @@ FP8X4 = mybir.dt.float8_e4m3fn_x4
 
 P = 128
 PACK = 4
-M_TILES = M // P
-HALF = S // 2
 LIST_COLS = S // 16
-HALF_COLS = LIST_COLS // 2
 
 
 def tile_list_tabhs_none_kernel(tc, tab, w, wgo, offs, offs2, out):
@@ -32,7 +29,6 @@ def tile_list_tabhs_none_kernel(tc, tab, w, wgo, offs, offs2, out):
     with ExitStack() as ctx:
         lists = ctx.enter_context(tc.tile_pool(name="lists", bufs=1))
         keep = ctx.enter_context(tc.tile_pool(name="keep", bufs=1))
-        turns = ctx.enter_context(tc.tile_pool(name="turns", bufs=1))
         psum = ctx.enter_context(tc.psum_pool(name="psum", bufs=1))
 
         pick = lists.tile([P, LIST_COLS], U16, name="pick")
@@ -41,11 +37,12 @@ def tile_list_tabhs_none_kernel(tc, tab, w, wgo, offs, offs2, out):
         words = keep.tile([P, T], U32, name="words", align_bytes=64)
         scales = keep.tile([P, T], U8, name="scales", align_bytes=64)
         weights_of_place = keep.tile([P, S], F32, name="weights_of_place", align_bytes=64)
-        w_raw_0a = keep.tile([P, 2, P], F32, name="w_raw_0a", align_bytes=64)
-        w_raw_0b = keep.tile([P, 2, P], F32, name="w_raw_0b", align_bytes=64)
+        w_low = keep.tile([P, 2, 2 * P], F32, name="w_low", align_bytes=64)
+        w_high = keep.tile([P, 2, 2 * P], F32, name="w_high", align_bytes=64)
+        w_raw_23 = keep.tile([P, PACK, 2 * P], F32, name="w_raw_23", tag="chain_b", align_bytes=64)
 
         nc.vector.memset(scales[:].bitcast(I32), 0)
-        nc.sync.dma_start(out=w_raw_0a[:], in_=w_rows[:, 0:2, 0:P])
+        nc.sync.dma_start(out=w_low[:], in_=w_rows[:, 0:2, 0 : 2 * P])
         nc.sync.dma_start(pick[:], offs)
         for quad in range(4):
             queue = nc.sync if quad < 3 else nc.scalar
@@ -53,14 +50,10 @@ def tile_list_tabhs_none_kernel(tc, tab, w, wgo, offs, offs2, out):
                 out=scales[32 * quad : 32 * quad + 4, :].bitcast(I32),
                 in_=tab_scales[4 * quad : 4 * quad + 4, :].bitcast(I32),
             )
-        nc.sync.dma_start(out=w_raw_0b[:], in_=w_rows[:, 2:4, 0:P])
+        nc.sync.dma_start(out=w_high[:], in_=w_rows[:, 2:4, 0 : 2 * P])
         nc.sync.dma_start(out=words[:].bitcast(I32), in_=tab_words.bitcast(I32))
-        w_raw_1 = turns.tile([P, PACK, P], F32, name="w_raw_1", offset=0, align_bytes=64)
-        nc.sync.dma_start(out=w_raw_1[:], in_=w_rows[:, :, P : 2 * P])
-        nc.gpsimd.dma_start(out=weights_of_place[:, 0:P], in_=wgo[:, 0:P])
         nc.sync.dma_start(place[:], offs2)
-        nc.sync.dma_start(out=weights_of_place[:, P:S], in_=wgo[:, P:S])
-        w_raw_23 = keep.tile([P, PACK, 2 * P], F32, name="w_raw_23", tag="chain_b", align_bytes=64)
+        nc.sync.dma_start(out=weights_of_place[:], in_=wgo)
         nc.sync.dma_start(out=w_raw_23[:], in_=w_rows[:, :, 2 * P : 4 * P])
         windows = []
         for i in range(3):
@@ -68,13 +61,11 @@ def tile_list_tabhs_none_kernel(tc, tab, w, wgo, offs, offs2, out):
             nc.vector.memset(window[:], 0.0)
             windows.append(window)
 
-        def interleave(name, raw, width, tag):
-            grouped = keep.tile([P, width, PACK], BF16, name=f"w_grouped{name}", tag=tag, align_bytes=64)
-            nc.scalar.copy(
-                grouped[:].rearrange("p (c i) j -> p c j i", i=PACK),
+        def interleave(copy, grouped, raw):
+            copy(
+                grouped.rearrange("p (c i) j -> p c j i", i=PACK),
                 raw.rearrange("p j (c i) -> p c j i", i=PACK),
             )
-            return grouped
 
         def quantize(name, grouped, width, tag):
             codes = keep.tile([P, width], U32, name=f"w_codes{name}", tag=tag, align_bytes=64)
@@ -92,11 +83,10 @@ def tile_list_tabhs_none_kernel(tc, tab, w, wgo, offs, offs2, out):
         def gather_words(lo, hi):
             nc.vector.tensor_copy(picked_words[:, lo:hi], words[:].indirect(pick[:, lo // 16 : hi // 16]))
 
-        def product(name, quantized, lo, hi):
+        def product(bank, quantized, lo, hi):
             codes, code_scales = quantized
-            bank = psum.tile([P, hi - lo], F32, name=f"bank{name}")
             nc.tensor.matmul_mx(
-                out=bank[:],
+                out=bank,
                 lhsT=codes.bitcast(FP8X4),
                 lhsT_scale=code_scales,
                 rhs=picked_words[:, lo:hi].bitcast(FP8X4),
@@ -104,14 +94,14 @@ def tile_list_tabhs_none_kernel(tc, tab, w, wgo, offs, offs2, out):
                 start=True,
                 stop=True,
             )
-            return bank
 
-        def result(name, width, tag):
-            return keep.tile([P, width], F32, name=f"y{name}", tag=tag, align_bytes=64)
-
-        def drained(name, bank, width, tag):
-            y = result(name, width, tag)
-            nc.scalar.copy(y[:], bank)
+        def result(name, quantized, cuts, tag):
+            lo, hi = cuts[0], cuts[-1]
+            bank = psum.tile([P, hi - lo], F32, name=f"bank{name}")
+            for a, b in zip(cuts[:-1], cuts[1:]):
+                product(bank[:, a - lo : b - lo], quantized, a, b)
+            y = keep.tile([P, hi - lo], F32, name=f"y{name}", tag=tag, align_bytes=64)
+            nc.scalar.copy(y[:], bank[:])
             return y[:]
 
         def scatter(window, y, lo, hi):
@@ -125,31 +115,33 @@ def tile_list_tabhs_none_kernel(tc, tab, w, wgo, offs, offs2, out):
         def store(m, window):
             nc.sync.dma_start(out=out[m * P : (m + 1) * P, :], in_=window[:])
 
-        nc.vector.tensor_copy(picked_scales[:], scales[:].indirect(pick[:]))
         grouped_0 = keep.tile([P, P, PACK], BF16, name="w_grouped0", align_bytes=64)
-        for half, raw in enumerate((w_raw_0a, w_raw_0b)):
-            nc.scalar.copy(
-                grouped_0[:, :, 2 * half : 2 * half + 2].rearrange("p (c i) j -> p c j i", i=PACK),
-                raw[:].rearrange("p j (c i) -> p c j i", i=PACK),
-            )
+        grouped_1 = keep.tile([P, P, PACK], BF16, name="w_grouped1", align_bytes=64)
+        interleave(nc.scalar.copy, grouped_0[:, :, 0:2], w_low[:, :, 0:P])
+        interleave(nc.vector.tensor_copy, grouped_1[:, :, 0:2], w_low[:, :, P : 2 * P])
+        nc.vector.tensor_copy(picked_scales[:], scales[:].indirect(pick[:]))
+        interleave(nc.scalar.copy, grouped_0[:, :, 2:4], w_high[:, :, 0:P])
+        interleave(nc.vector.tensor_copy, grouped_1[:, :, 2:4], w_high[:, :, P : 2 * P])
         q0 = quantize("0", grouped_0, P, "codes_0")
+        q1 = quantize("1", grouped_1, P, "chain_c")
         gather_words(0, P)
-        gather_words(P, S)
-        scatter(windows[0], drained("0a", product("0a", q0, 0, P)[:], P, "y0a"), 0, P)
-        q1 = quantize("1", interleave("1", w_raw_1[:], P, "grouped_1"), P, "chain_c")
-        y0b = turns.tile([P, HALF], F32, name="y0b", offset=0, align_bytes=64)
-        nc.scalar.copy(y0b[:], product("0b", q0, P, 3 * P)[:])
-        scatter(windows[0], y0b[:], P, 3 * P)
-        scatter(windows[1], drained("1a", product("1a", q1, 0, HALF)[:], HALF, "y1a"), 0, HALF)
-        c23, s23 = quantize("23", interleave("23", w_raw_23[:], 2 * P, "chain_c"), 2 * P, "codes_23")
-        late = result("late", 3 * P, "chain_b")
-        nc.scalar.copy(late[:, 0:P], product("0c", q0, 3 * P, S)[:])
-        scatter(windows[0], late[:, 0:P], 3 * P, S)
+        gather_words(P, 3 * P)
+        gather_words(3 * P, S)
+        scatter(windows[0], result("0a", q0, (0, P), "y0a"), 0, P)
+        scatter(windows[1], result("1a", q1, (0, P), "y1a"), 0, P)
+        scatter(windows[0], result("0b", q0, (P, 3 * P, S), "y0b"), P, S)
         store(0, windows[0])
-        nc.scalar.copy(late[:, P : 3 * P], product("1b", q1, HALF, S)[:])
-        scatter(windows[1], late[:, P : 3 * P], HALF, S)
+        bank_1b = psum.tile([P, 3 * P], F32, name="bank1b")
+        product(bank_1b[:, 0 : 2 * P], q1, P, 3 * P)
+        product(bank_1b[:, 2 * P : 3 * P], q1, 3 * P, S)
+        grouped_23 = keep.tile([P, 2 * P, PACK], BF16, name="w_grouped23", tag="chain_c", align_bytes=64)
+        interleave(nc.scalar.copy, grouped_23[:], w_raw_23[:])
+        c23, s23 = quantize("23", grouped_23, 2 * P, "codes_23")
+        y1b = keep.tile([P, 3 * P], F32, name="y1b", tag="chain_b", align_bytes=64)
+        nc.scalar.copy(y1b[:], bank_1b[:])
+        scatter(windows[1], y1b[:], P, S)
         store(1, windows[1])
-        scatter(windows[2], drained("2", product("2", (c23[:, 0:P], s23[:, 0:P]), 0, S)[:], S, "y2"), 0, S)
+        scatter(windows[2], result("2", (c23[:, 0:P], s23[:, 0:P]), (0, S), "y2"), 0, S)
         store(2, windows[2])
-        scatter(windows[0], drained("3", product("3", (c23[:, P : 2 * P], s23[:, P : 2 * P]), 0, S)[:], S, "y3"), 0, S)
+        scatter(windows[0], result("3", (c23[:, P : 2 * P], s23[:, P : 2 * P]), (0, S), "y3"), 0, S)
         store(3, windows[0])

@@ -29,6 +29,7 @@ def tile_list_tabhs_none_kernel(tc, tab, w, wgo, offs, offs2, out):
     with ExitStack() as ctx:
         lists = ctx.enter_context(tc.tile_pool(name="lists", bufs=1))
         keep = ctx.enter_context(tc.tile_pool(name="keep", bufs=1))
+        turns = ctx.enter_context(tc.tile_pool(name="turns", bufs=1))
         psum = ctx.enter_context(tc.psum_pool(name="psum", bufs=1))
 
         pick = lists.tile([P, LIST_COLS], U16, name="pick")
@@ -38,7 +39,8 @@ def tile_list_tabhs_none_kernel(tc, tab, w, wgo, offs, offs2, out):
         scales = keep.tile([P, T], U8, name="scales", align_bytes=64)
         weights_of_place = keep.tile([P, S], F32, name="weights_of_place", align_bytes=64)
         w_low = keep.tile([P, 2, 2 * P], F32, name="w_low", align_bytes=64)
-        w_high = keep.tile([P, 2, 2 * P], F32, name="w_high", align_bytes=64)
+        w_high_0 = keep.tile([P, 2, P], F32, name="w_high_0", align_bytes=64)
+        w_high_1 = turns.tile([P, 2, P], F32, name="w_high_1", offset=0, align_bytes=64)
         w_raw_23 = keep.tile([P, PACK, 2 * P], F32, name="w_raw_23", tag="chain_b", align_bytes=64)
 
         nc.vector.memset(scales[:].bitcast(I32), 0)
@@ -50,8 +52,9 @@ def tile_list_tabhs_none_kernel(tc, tab, w, wgo, offs, offs2, out):
                 out=scales[32 * quad : 32 * quad + 4, :].bitcast(I32),
                 in_=tab_scales[4 * quad : 4 * quad + 4, :].bitcast(I32),
             )
-        nc.sync.dma_start(out=w_high[:], in_=w_rows[:, 2:4, 0 : 2 * P])
+        nc.sync.dma_start(out=w_high_0[:], in_=w_rows[:, 2:4, 0:P])
         nc.sync.dma_start(out=words[:].bitcast(I32), in_=tab_words.bitcast(I32))
+        nc.sync.dma_start(out=w_high_1[:], in_=w_rows[:, 2:4, P : 2 * P])
         nc.sync.dma_start(place[:], offs2)
         nc.sync.dma_start(out=weights_of_place[:], in_=wgo)
         nc.sync.dma_start(out=w_raw_23[:], in_=w_rows[:, :, 2 * P : 4 * P])
@@ -95,12 +98,12 @@ def tile_list_tabhs_none_kernel(tc, tab, w, wgo, offs, offs2, out):
                 stop=True,
             )
 
-        def result(name, quantized, cuts, tag):
+        def result(name, quantized, cuts, offset):
             lo, hi = cuts[0], cuts[-1]
-            bank = psum.tile([P, hi - lo], F32, name=f"bank{name}")
+            bank = psum.tile([P, hi - lo], F32, name=f"bank{name}", tag=f"bank{name}")
             for a, b in zip(cuts[:-1], cuts[1:]):
                 product(bank[:, a - lo : b - lo], quantized, a, b)
-            y = keep.tile([P, hi - lo], F32, name=f"y{name}", tag=tag, align_bytes=64)
+            y = turns.tile([P, hi - lo], F32, name=f"y{name}", offset=offset, align_bytes=64)
             nc.scalar.copy(y[:], bank[:])
             return y[:]
 
@@ -120,16 +123,21 @@ def tile_list_tabhs_none_kernel(tc, tab, w, wgo, offs, offs2, out):
         interleave(nc.scalar.copy, grouped_0[:, :, 0:2], w_low[:, :, 0:P])
         interleave(nc.vector.tensor_copy, grouped_1[:, :, 0:2], w_low[:, :, P : 2 * P])
         nc.vector.tensor_copy(picked_scales[:], scales[:].indirect(pick[:]))
-        interleave(nc.scalar.copy, grouped_0[:, :, 2:4], w_high[:, :, 0:P])
-        interleave(nc.vector.tensor_copy, grouped_1[:, :, 2:4], w_high[:, :, P : 2 * P])
+        interleave(nc.scalar.copy, grouped_0[:, :, 2:4], w_high_0[:])
         q0 = quantize("0", grouped_0, P, "codes_0")
-        q1 = quantize("1", grouped_1, P, "chain_c")
         gather_words(0, P)
         gather_words(P, 3 * P)
         gather_words(3 * P, S)
-        scatter(windows[0], result("0a", q0, (0, P), "y0a"), 0, P)
-        scatter(windows[1], result("1a", q1, (0, P), "y1a"), 0, P)
-        scatter(windows[0], result("0b", q0, (P, 3 * P, S), "y0b"), P, S)
+        interleave(nc.scalar.copy, grouped_1[:, :, 2:4], w_high_1[:])
+        q1 = quantize("1", grouped_1, P, "chain_c")
+        scatter(windows[0], result("0a", q0, (0, P), 0), 0, P)
+        scatter(windows[1], result("1a", q1, (0, P), 2048), 0, P)
+        y0b = turns.tile([P, 3 * P], F32, name="y0b", offset=512, align_bytes=64)
+        for lo, hi in ((P, 3 * P), (3 * P, S)):
+            bank_0 = psum.tile([P, hi - lo], F32, name=f"bank0_{lo}", tag="bank0b" if lo == P else "bank0a")
+            product(bank_0[:], q0, lo, hi)
+            nc.scalar.copy(y0b[:, lo - P : hi - P], bank_0[:])
+        scatter(windows[0], y0b[:], P, S)
         store(0, windows[0])
         bank_1b = psum.tile([P, 3 * P], F32, name="bank1b")
         product(bank_1b[:, 0 : 2 * P], q1, P, 3 * P)
@@ -141,7 +149,7 @@ def tile_list_tabhs_none_kernel(tc, tab, w, wgo, offs, offs2, out):
         nc.scalar.copy(y1b[:], bank_1b[:])
         scatter(windows[1], y1b[:], P, S)
         store(1, windows[1])
-        scatter(windows[2], result("2", (c23[:, 0:P], s23[:, 0:P]), (0, S), "y2"), 0, S)
+        scatter(windows[2], result("2", (c23[:, 0:P], s23[:, 0:P]), (0, S), 2560), 0, S)
         store(2, windows[2])
-        scatter(windows[0], result("3", (c23[:, P : 2 * P], s23[:, P : 2 * P]), (0, S), "y3"), 0, S)
+        scatter(windows[0], result("3", (c23[:, P : 2 * P], s23[:, P : 2 * P]), (0, S), 4608), 0, S)
         store(3, windows[0])

@@ -16,6 +16,7 @@ FP8X4 = mybir.dt.float8_e4m3fn_x4
 P = 128
 PACK = 4
 LIST_COLS = S // 16
+FIRST = 192
 
 
 def tile_list_tabhs_none_kernel(tc, tab, w, wgo, offs, offs2, out):
@@ -126,18 +127,23 @@ def tile_list_tabhs_none_kernel(tc, tab, w, wgo, offs, offs2, out):
         interleave(nc.scalar.copy, grouped_0[:, :, 2:4], w_high_0[:])
         q0 = quantize("0", grouped_0, P, "codes_0")
         gather_words(0, P)
-        gather_words(P, 3 * P)
-        gather_words(3 * P, S)
+        gather_words(P, FIRST)
+        gather_words(FIRST, S)
         interleave(nc.scalar.copy, grouped_1[:, :, 2:4], w_high_1[:])
         q1 = quantize("1", grouped_1, P, "chain_c")
-        scatter(windows[0], result("0a", q0, (0, P), 0), 0, P)
-        scatter(windows[1], result("1a", q1, (0, P), 2048), 0, P)
-        y0b = turns.tile([P, 3 * P], F32, name="y0b", offset=512, align_bytes=64)
-        for lo, hi in ((P, 3 * P), (3 * P, S)):
-            bank_0 = psum.tile([P, hi - lo], F32, name=f"bank0_{lo}", tag="bank0b" if lo == P else "bank0a")
+        y0a = turns.tile([P, FIRST], F32, name="y0a", offset=0, align_bytes=64)
+        for lo, hi in ((0, P), (P, FIRST)):
+            bank_0 = psum.tile([P, hi - lo], F32, name=f"bank0_{lo}", tag=f"bank0_{lo}")
             product(bank_0[:], q0, lo, hi)
-            nc.scalar.copy(y0b[:, lo - P : hi - P], bank_0[:])
-        scatter(windows[0], y0b[:], P, S)
+            nc.scalar.copy(y0a[:, lo:hi], bank_0[:])
+        scatter(windows[0], y0a[:], 0, FIRST)
+        scatter(windows[1], result("1a", q1, (0, P), 2048), 0, P)
+        y0b = turns.tile([P, S - FIRST], F32, name="y0b", offset=768, align_bytes=64)
+        for lo, hi in ((FIRST, 2 * P), (2 * P, S)):
+            bank_0 = psum.tile([P, hi - lo], F32, name=f"bank0_{lo}", tag="bank0b" if lo == FIRST else "bank0_0")
+            product(bank_0[:], q0, lo, hi)
+            nc.scalar.copy(y0b[:, lo - FIRST : hi - FIRST], bank_0[:])
+        scatter(windows[0], y0b[:], FIRST, S)
         store(0, windows[0])
         bank_1b = psum.tile([P, 3 * P], F32, name="bank1b")
         product(bank_1b[:, 0 : 2 * P], q1, P, 3 * P)

@@ -126,13 +126,14 @@ def tile_list_tabhs_none_kernel(tc, tab, w, wgo, offs, offs2, out):
         nc.vector.tensor_copy(picked_scales[:], scales[:].indirect(pick[:]))
         interleave(nc.scalar.copy, grouped_0[:, :, 2:4], w_high_0[:])
         q0 = quantize("0", grouped_0, P, "codes_0")
-        gather_words(0, P)
-        gather_words(P, FIRST)
+        first_cuts = [(lo, lo + 64) for lo in range(0, FIRST, 64)]
+        for lo, hi in first_cuts:
+            gather_words(lo, hi)
         gather_words(FIRST, S)
         interleave(nc.scalar.copy, grouped_1[:, :, 2:4], w_high_1[:])
         q1 = quantize("1", grouped_1, P, "chain_c")
         y0a = turns.tile([P, FIRST], F32, name="y0a", offset=0, align_bytes=64)
-        for lo, hi in ((0, P), (P, FIRST)):
+        for lo, hi in first_cuts:
             bank_0 = psum.tile([P, hi - lo], F32, name=f"bank0_{lo}", tag=f"bank0_{lo}")
             product(bank_0[:], q0, lo, hi)
             nc.scalar.copy(y0a[:, lo:hi], bank_0[:])

from contextlib import ExitStack

import concourse.mybir as mybir

K, M, T, S = 512, 512, 1024, 512
FLOPS = 2 * K * M * S

F32 = mybir.dt.float32
BF16 = mybir.dt.bfloat16
I32 = mybir.dt.int32
U32 = mybir.dt.uint32
U16 = mybir.dt.uint16
U8 = mybir.dt.uint8
FP8X4 = mybir.dt.float8_e4m3fn_x4

P = 128
PACK = 4
LIST_COLS = S // 16
FIRST = 192


def tile_list_tabhs_none_kernel(tc, tab, w, wgo, offs, offs2, out):
    nc = tc.nc
    mult = mybir.AluOpType.mult

    tab_words = tab[0, 0 : 4 * P * T].rearrange("(p n) -> p n", p=P)
    tab_scales = tab[0, 4 * P * T :].rearrange("(q n) -> q n", q=16)
    w_rows = w.rearrange("(p j) c -> p j c", j=PACK)

    with ExitStack() as ctx:
        lists = ctx.enter_context(tc.tile_pool(name="lists", bufs=1))
        keep = ctx.enter_context(tc.tile_pool(name="keep", bufs=1))
        turns = ctx.enter_context(tc.tile_pool(name="turns", bufs=1))
        psum = ctx.enter_context(tc.psum_pool(name="psum", bufs=1))

        pick = lists.tile([P, LIST_COLS], U16, name="pick")
        place = lists.tile([P, LIST_COLS], U16, name="place")

        words = keep.tile([P, T], U32, name="words", align_bytes=64)
        scales = keep.tile([P, T], U8, name="scales", align_bytes=64)
        weights_of_place = keep.tile([P, S], F32, name="weights_of_place", align_bytes=64)
        w_low = keep.tile([P, 2, 2 * P], F32, name="w_low", align_bytes=64)
        w_high_0 = keep.tile([P, 2, P], F32, name="w_high_0", align_bytes=64)
        w_high_1 = turns.tile([P, 2, P], F32, name="w_high_1", offset=0, align_bytes=64)
        w_raw_23 = keep.tile([P, PACK, 2 * P], F32, name="w_raw_23", tag="chain_b", align_bytes=64)

        nc.vector.memset(scales[:].bitcast(I32), 0)
        nc.sync.dma_start(out=w_low[:], in_=w_rows[:, 0:2, 0 : 2 * P])
        nc.sync.dma_start(pick[:], offs)
        for quad in range(4):
            queue = nc.sync if quad < 3 else nc.scalar
            queue.dma_start(
                out=scales[32 * quad : 32 * quad + 4, :].bitcast(I32),
                in_=tab_scales[4 * quad : 4 * quad + 4, :].bitcast(I32),
            )
        nc.sync.dma_start(out=w_high_0[:], in_=w_rows[:, 2:4, 0:P])
        nc.sync.dma_start(out=words[:].bitcast(I32), in_=tab_words.bitcast(I32))
        nc.sync.dma_start(out=w_high_1[:], in_=w_rows[:, 2:4, P : 2 * P])
        nc.sync.dma_start(place[:], offs2)
        nc.sync.dma_start(out=weights_of_place[:], in_=wgo)
        nc.sync.dma_start(out=w_raw_23[:], in_=w_rows[:, :, 2 * P : 4 * P])
        windows = []
        for i in range(3):
            window = keep.tile([P, T], F32, name=f"window{i}", align_bytes=64)
            nc.vector.memset(window[:], 0.0)
            windows.append(window)

        def interleave(copy, grouped, raw):
            copy(
                grouped.rearrange("p (c i) j -> p c j i", i=PACK),
                raw.rearrange("p j (c i) -> p c j i", i=PACK),
            )

        def quantize(name, grouped, width, tag):
            codes = keep.tile([P, width], U32, name=f"w_codes{name}", tag=tag, align_bytes=64)
            code_scales = keep.tile([P, width], U8, name=f"w_scales{name}", align_bytes=64)
            nc.vector.quantize_mx(
                out=codes[:].bitcast(FP8X4),
                scales=code_scales[:],
                in_=grouped[:].rearrange("p c j -> p (c j)"),
            )
            return codes[:], code_scales[:]

        picked_scales = keep.tile([P, S], U8, name="picked_scales", align_bytes=64)
        picked_words = keep.tile([P, S], U32, name="picked_words", align_bytes=64)

        def gather_words(lo, hi):
            nc.vector.tensor_copy(picked_words[:, lo:hi], words[:].indirect(pick[:, lo // 16 : hi // 16]))

        def product(bank, quantized, lo, hi):
            codes, code_scales = quantized
            nc.tensor.matmul_mx(
                out=bank,
                lhsT=codes.bitcast(FP8X4),
                lhsT_scale=code_scales,
                rhs=picked_words[:, lo:hi].bitcast(FP8X4),
                rhs_scale=picked_scales[:, lo:hi],
                start=True,
                stop=True,
            )

        def result(name, quantized, cuts, offset):
            lo, hi = cuts[0], cuts[-1]
            bank = psum.tile([P, hi - lo], F32, name=f"bank{name}", tag=f"bank{name}")
            for a, b in zip(cuts[:-1], cuts[1:]):
                product(bank[:, a - lo : b - lo], quantized, a, b)
            y = turns.tile([P, hi - lo], F32, name=f"y{name}", offset=offset, align_bytes=64)
            nc.scalar.copy(y[:], bank[:])
            return y[:]

        def scatter(window, y, lo, hi):
            nc.vector.tensor_tensor(
                window[:].indirect(place[:, lo // 16 : hi // 16]),
                y,
                weights_of_place[:, lo:hi],
                mult,
            )

        def store(m, window):
            nc.sync.dma_start(out=out[m * P : (m + 1) * P, :], in_=window[:])

        grouped_0 = keep.tile([P, P, PACK], BF16, name="w_grouped0", align_bytes=64)
        grouped_1 = keep.tile([P, P, PACK], BF16, name="w_grouped1", align_bytes=64)
        interleave(nc.scalar.copy, grouped_0[:, :, 0:2], w_low[:, :, 0:P])
        interleave(nc.vector.tensor_copy, grouped_1[:, :, 0:2], w_low[:, :, P : 2 * P])
        nc.vector.tensor_copy(picked_scales[:], scales[:].indirect(pick[:]))
        interleave(nc.scalar.copy, grouped_0[:, :, 2:4], w_high_0[:])
        q0 = quantize("0", grouped_0, P, "codes_0")
        first_cuts = [(lo, lo + 64) for lo in range(0, FIRST, 64)]
        for lo, hi in first_cuts:
            gather_words(lo, hi)
        gather_words(FIRST, S)
        interleave(nc.scalar.copy, grouped_1[:, :, 2:4], w_high_1[:])
        q1 = quantize("1", grouped_1, P, "chain_c")
        y0a = turns.tile([P, FIRST], F32, name="y0a", offset=0, align_bytes=64)
        for lo, hi in first_cuts:
            bank_0 = psum.tile([P, hi - lo], F32, name=f"bank0_{lo}", tag=f"bank0_{lo}")
            product(bank_0[:], q0, lo, hi)
            nc.scalar.copy(y0a[:, lo:hi], bank_0[:])
        scatter(windows[0], y0a[:], 0, FIRST)
        scatter(windows[1], result("1a", q1, (0, P), 2048), 0, P)
        y0b = turns.tile([P, S - FIRST], F32, name="y0b", offset=768, align_bytes=64)
        for lo, hi in ((FIRST, 2 * P), (2 * P, S)):
            bank_0 = psum.tile([P, hi - lo], F32, name=f"bank0_{lo}", tag="bank0b" if lo == FIRST else "bank0_0")
            product(bank_0[:], q0, lo, hi)
            nc.scalar.copy(y0b[:, lo - FIRST : hi - FIRST], bank_0[:])
        scatter(windows[0], y0b[:], FIRST, S)
        store(0, windows[0])
        bank_1b = psum.tile([P, 3 * P], F32, name="bank1b")
        product(bank_1b[:, 0 : 2 * P], q1, P, 3 * P)
        product(bank_1b[:, 2 * P : 3 * P], q1, 3 * P, S)
        grouped_23 = keep.tile([P, 2 * P, PACK], BF16, name="w_grouped23", tag="chain_c", align_bytes=64)
        interleave(nc.scalar.copy, grouped_23[:], w_raw_23[:])
        c23, s23 = quantize("23", grouped_23, 2 * P, "codes_23")
        y1b = keep.tile([P, 3 * P], F32, name="y1b", tag="chain_b", align_bytes=64)
        nc.scalar.copy(y1b[:], bank_1b[:])
        scatter(windows[1], y1b[:], P, S)
        store(1, windows[1])
        scatter(windows[2], result("2", (c23[:, 0:P], s23[:, 0:P]), (0, S), 2560), 0, S)
        store(2, windows[2])
        scatter(windows[0], result("3", (c23[:, P : 2 * P], s23[:, P : 2 * P]), (0, S), 4608), 0, S)
        store(3, windows[0])
